import numpy as np, ml_dtypes
CORES = [16,17,18,19,32,33,34,35]
N = 8
BF = ml_dtypes.bfloat16
W, S, B, M = 4096, 1024, 4, 5
def dot(a, x):
    return np.add.reduce(a[:, :, None] * x, axis=1)
def put(w, a, x):
    z = B * np.arange(S) + (dot(a, x) & (B - 1))
    np.put_along_axis(w, z[:, None, :], x, 2)
def pack(b, e, q):
    return {"tab": b.reshape(N, 128, W).astype(np.float32).astype(BF), "res": e.reshape(N, 128, M * S).astype(np.float32).astype(BF), "hw": q.reshape(N, 128, 3).astype(np.float32).astype(BF)}
def parts(rng):
    return rng.integers(0, 256, (N, 8, 16, W)), rng.integers(0, 256, (N, 8, 16, M, S)), rng.integers(0, 256, (N, 8, 16, 3))
def store(b, x, q):
    e = np.array(x)
    for r in range(N):
        w = np.array(b[r])
        for t in range(M):
            if t > 0:
                h = dot(q[r, :, :, 0], x[r, :, :, t - 1])
                if r > 0: h = h + dot(q[r - 1, :, :, 1], x[r - 1, :, :, t])
                e[r, :, :, t] = (x[r, :, :, t] - np.take_along_axis(w, (h & (W - 1))[:, None, :], 2)) & 255
            put(w, q[r, :, :, 2], x[r, :, :, t])
    return e
def plant(rng, goal, code):
    b, x, q = parts(rng)
    q[:, :, 0, 0] = 1; q[:, :, 1, 0] = 128; q[:, :, :2, 2] = 16 * rng.integers(0, 16, (N, 8, 2)); q[:, :, 2, 2] = 1
    for r in range(N):
        for t in range(M):
            rest = dot(q[r, :, 3:, 2], x[r, :, 3:, t])
            x[r, :, 2, t] = B * rng.integers(0, 256 // B, (8, S)) + ((code[r, :, t] - rest) & (B - 1))
            if t + 1 < M:
                d = goal[r, :, t + 1] - dot(q[r, :, 2:, 0], x[r, :, 2:, t])
                if r > 0: d = d - dot(q[r - 1, :, :, 1], x[r - 1, :, :, t + 1])
                d = d & (W - 1); x[r, :, 0, t] = d & 127; x[r, :, 1, t] = d >> 7
    return pack(b, store(b, x, q), q)
def chase(rng, code, lag):
    o = rng.integers(0, S, code.shape); t = np.maximum(np.arange(M)[None, None, :, None] - lag, 0)
    return B * o + code[np.arange(N)[:, None, None, None], np.arange(8)[None, :, None, None], t, o]
def setup_inputs(rng):
    return pack(*parts(rng))
def setup_inputs_fresh(rng):
    code = rng.integers(0, B, (N, 8, M, S)); code = np.where(rng.random((N, 8, 1, S)) < 0.5, code[:, :, :1], code)
    a = rng.permutation(N)[:2]; t = np.arange(M)[None, :, None]
    code[a] = (rng.integers(0, B, (2, 8, 1, S)) + t[None] * (1 + 2 * rng.integers(0, B // 2, (2, 8, 1, S)))) & (B - 1)
    goal = chase(rng, code, rng.integers(1, M, code.shape)); goal[:, ::4, 1:] = B * np.arange(S) + code[:, ::4, :-1]
    goal = np.where(rng.random(code.shape) < 0.1, rng.integers(0, W, code.shape), goal)
    one = np.maximum(t - 1, 0) + np.zeros((8, M, S), np.int64)
    two = np.floor(rng.random((8, M, S)) * np.maximum(t - 1, 1)).astype(np.int64)
    for i, came in ((0, one), (1, two)):
        o = np.argsort(rng.random((8, M, S)), axis=-1)
        goal[a[i]] = B * o + code[a[i]][np.arange(8)[:, None, None], came, o]
    return plant(rng, goal, code)
def setup_inputs_same(rng):
    code = (rng.integers(0, B, (N, 8, 1, S)) + np.arange(M)[None, None, :, None] * rng.integers(1, B, (N, 8, 1, S))) & (B - 1)
    return plant(rng, chase(rng, code, rng.integers(0, 2, code.shape)), code)
def setup_inputs_alike(rng):
    goal = rng.integers(0, W, (N, 8, M, S)); code = rng.integers(0, B, (N, 8, M, S)); p = rng.permutation(8); last = S * B - 1
    goal[:, p[0]] = 0; goal[:, p[1]] = W - 1; goal[:, p[2]] = last; goal[:, p[3]] = S * B if S * B < W else W // 2
    goal[:, p[4]] = np.argsort(rng.random((N, M, W)), axis=-1)[..., :S]
    goal[:, p[5]] = rng.choice(np.array([0, B - 1, B, last]), (N, M, S))
    goal[:, p[6]] = B * np.arange(S) + rng.integers(0, B, (N, M, S))
    code[:, p[0]] = 0; code[:, p[2]] = B - 1; code[:, p[5]] = code[:, p[5], :1]
    goal[rng.integers(0, N)] = (W // 4) * rng.integers(0, 4, (1, M, 1)) + np.argsort(rng.random((8, M, W // 4)), axis=-1)[..., :S]
    return plant(rng, goal, code)
def setup_inputs_ends(rng):
    b, x, q = parts(rng); p = rng.permutation(8)
    q[:, p[0], :, 0] = 0; q[:, p[1], :, 1] = 0; q[:, p[2]] = 255; x[:, p[2]] = 255; q[:, p[3], :, 2] = 0; q[:, p[4]] = 0
    q[:, p[3], :, :2] = rng.integers(200, 256, (N, 16, 2))
    x[:, p[3]] = 255 - np.floor(rng.random((N, 16, M, S)) * rng.integers(56, 257, (N, 1, M, S))).astype(np.int64)
    x[:, p[5]] = 255 * rng.integers(0, 2, (N, 16, M, S))
    b[:, p[6]] = 255; x[:, p[6]] = rng.choice(np.array([0, 1, 254, 255]), (N, 16, M, S))
    x[:, p[7]] = x[:, p[7]] * (rng.random((N, 16, M, S)) < 0.1); q[:, p[7]] = rng.choice(np.array([0, 1, 128, 255]), (N, 16, 3))
    return pack(b, store(b, x, q), q)
def uneven(rng, *shape):
    return np.floor(rng.random(shape) * np.exp2(rng.integers(0, 9, (N, 8, 1) + shape[3:]))).astype(np.int64)
def setup_inputs_spread(rng):
    q = np.floor(rng.random((N, 8, 16, 3)) * np.exp2(rng.integers(0, 9, (N, 8, 16, 3)))).astype(np.int64)
    return pack(uneven(rng, N, 8, 16, W), uneven(rng, N, 8, 16, M, S), q)
def check_inputs(d):
    bad = []
    for k in ("tab", "res", "hw"):
        a = np.asarray(d[k]).astype(np.float32)
        if not np.all((a >= 0) & (a <= 255) & (a == np.floor(a))): bad.append("whole numbers from 0 to 255 in " + k)
    return bad
def reference(tab, res, hw):
    b = tab.astype(np.float32).astype(np.int64).reshape(N, 8, 16, W)
    e = res.astype(np.float32).astype(np.int64).reshape(N, 8, 16, M, S)
    q = hw.astype(np.float32).astype(np.int64).reshape(N, 8, 16, 3)
    y = np.zeros((N, 8, 16, M, S), np.int64)
    for r in range(N):
        w = np.array(b[r])
        for t in range(M):
            x = e[r, :, :, t]
            if t > 0:
                h = dot(q[r, :, :, 0], y[r, :, :, t - 1])
                if r > 0: h = h + dot(q[r - 1, :, :, 1], y[r - 1, :, :, t])
                x = (np.take_along_axis(w, (h & (W - 1))[:, None, :], 2) + x) & 255
            y[r, :, :, t] = x
            put(w, q[r, :, :, 2], x)
    return {"y": y.reshape(N, 128, M * S).astype(np.float32).astype(BF)}

@@ -1,0 +1,382 @@
+from concourse.mybir import AluOpType as ALU, ActivationFunctionType as ACT
+
+S, M, W, NC = 1024, 5, 4096, 64
+LIFT = 256.25
+
+CFG = {
+    "chunks": [0, 16, 32, 48, 64],
+    "w1": 32,
+    "u1": 48,
+    "w1_late": False,
+    "pieces": [(0, 24, "a"), (24, 32, "v"), (32, 52, "a"), (52, 64, "v")],
+    "tab": [(0, 8, "a", "v"), (8, 24, "a", "v"), (24, 40, "a", "v"), (40, 52, "a", "a"), (52, 64, "v", "v")],
+    "res0_at": 1,
+    "early0": 2,
+    "far_v": (0, 2),
+}
+MAXC = 8
+
+SCRATCH = {
+    "R": ("sbuf", [128, M * S], "bfloat16"),
+    "Z": ("sbuf", [128, (M - 1) * S], "bfloat16"),
+    "tb": ("sbuf", [128, W], "bfloat16"),
+    "tf": ("sbuf", [128, W], "float32"),
+    "hwb": ("sbuf", [128, 8], "bfloat16"),
+    "Ub": ("sbuf", [128, 144], "bfloat16"),
+    "Wb": ("sbuf", [128, 144], "bfloat16"),
+    "Vb": ("sbuf", [128, 144], "bfloat16"),
+    "Vin": ("sbuf", [128, 144], "bfloat16"),
+    "i8": ("sbuf", [128, 8], "int32"),
+    "p4i": ("sbuf", [128, 4], "int32"),
+    "p4f": ("sbuf", [128, 4], "float32"),
+    "jc0": ("sbuf", [128, NC], "int32"),
+    "jc1": ("sbuf", [128, NC], "int32"),
+    "s32": ("sbuf", [128, S], "int32"),
+    "xs": ("sbuf", [128, S], "float32"),
+    "us": ("sbuf", [128, 2 * NC], "float32"),
+    "vo": ("sbuf", [128, (M - 1) * NC], "float32"),
+    "vl": ("sbuf", [128, (M - 1) * NC], "float32"),
+    "ha": ("sbuf", [128, NC], "int32"),
+    "ho": ("sbuf", [128, NC], "uint16"),
+    "wa": ("sbuf", [128, NC], "int32"),
+    "wo": ("sbuf", [128, NC], "uint16"),
+    "pv0": ("psum", [128, 512], "float32"),
+    "pv1": ("psum", [128, 512], "float32"),
+    "pw0": ("psum", [128, 512], "float32"),
+    "pw1": ("psum", [128, 512], "float32"),
+    "pu0": ("psum", [128, 512], "float32"),
+    "pu1": ("psum", [128, 512], "float32"),
+    "px0": ("psum", [128, 512], "float32"),
+    "px1": ("psum", [128, 512], "float32"),
+}
+POOL = {"d": 34, "v": 16, "a": 22, "p": 22, "g": 12}
+SEMAPHORES = ([k + str(i) for k in POOL for i in range(POOL[k])]
+              + ["z%d_%d" % (t, c) for t in range(1, M) for c in range(MAXC)] + ["vin"] + ["sent%d" % t for t in range(M)])
+
+
+def rg(name, a, b):
+    return [(name, c) for c in range(a, b)]
+
+
+def emit(g, T, ops):
+    queues = {"g": g, "v": g.vector, "a": g.scalar, "p": g.tensor, "s": g.sync}
+    last, total = {}, {}
+    for k, o in enumerate(ops):
+        if o["tok"] is None and o["waited"]:
+            pool = "d" if o["dma"] else o["q"]
+            for i in range(POOL[pool]):
+                s = pool + str(i)
+                if s not in last or o["kn"] >> last[s] & 1:
+                    break
+            else:
+                raise ValueError("out of semaphores in pool " + pool)
+            last[s] = k
+            total[s] = total.get(s, 0) + (16 if o["dma"] else 1)
+            o["tok"] = (s, total[s])
+            o["inc"] = True
+    for o in ops:
+        if o["q"] is None:
+            continue
+        q = queues[o["q"]]
+        for d in o["waits"]:
+            q.wait_ge(T.sem[ops[d]["tok"][0]], ops[d]["tok"][1])
+        if o["fn"] is not None:
+            ins = o["fn"]()
+            if o["inc"]:
+                ins.then_inc(T.sem[o["tok"][0]], 16 if o["dma"] else 1)
+
+
+def rank_program(g, core, T, topo):
+    rank = T.rank_of(core)
+    if rank is None:
+        return
+    n = len(T.cores)
+    up = T.cores[rank + 1] if rank + 1 < n else None
+    down = T.cores[rank - 1] if rank > 0 else None
+    ch = list(zip(CFG["chunks"], CFG["chunks"][1:]))
+    w1, u1, pieces, tabp = CFG["w1"], CFG["u1"], CFG["pieces"], CFG["tab"]
+    far_up = CFG["far_v"] if up is not None and topo.chip(up) != topo.chip(core) else ()
+    far_down = CFG["far_v"] if down is not None and topo.chip(down) != topo.chip(core) else ()
+
+    ops, known, writer, readers = [], {}, {}, {}
+
+    def op(q, fn, reads=(), writes=(), dma=False, after=()):
+        k = len(ops)
+        deps = set(after)
+        for r in reads:
+            if r in writer:
+                deps.add(writer[r])
+        for r in writes:
+            if r in writer:
+                deps.add(writer[r])
+            deps.update(readers.get(r, ()))
+        kn, waits = known.get(q, 0), []
+        for d in sorted(deps, reverse=True):
+            if not kn >> d & 1:
+                waits.append(d)
+                ops[d]["waited"] = True
+                kn |= ops[d]["kn"] | 1 << d
+        known[q] = kn
+        ops.append({"q": q, "fn": fn, "waits": waits[::-1], "kn": kn, "dma": dma, "waited": False, "tok": None, "inc": False})
+        for r in reads:
+            readers.setdefault(r, []).append(k)
+        for r in writes:
+            writer[r] = k
+            readers[r] = []
+        return k
+
+    def ext(sem, val, writes=(), kn=0):
+        k = len(ops)
+        ops.append({"q": None, "fn": None, "waits": [], "kn": kn, "dma": False, "waited": False, "tok": (sem, val), "inc": False})
+        for r in writes:
+            writer[r] = k
+            readers[r] = []
+        return k
+
+    V, A, P, Y = g.vector, g.scalar, g.tensor, g.sync
+    ends = []
+
+    def xr(t, a, b):
+        return rg("R%d" % t, a, b)
+
+    def xc(t, a, b):
+        return T.R[:, t * S + 16 * a:t * S + 16 * b]
+
+    def load(q, out, in_, writes, after=()):
+        e = A if q == "a" else Y
+        return op(q, lambda: e.dma_start(out, in_), writes=writes, dma=True, after=after)
+
+    def load_res(t, after=()):
+        cut = [0, ch[0][1], NC] if t == 1 else [0, NC]
+        for a, b in zip(cut, cut[1:]):
+            load("s", xc(t, a, b), T.res[:, t * S + 16 * a:t * S + 16 * b], xr(t, a, b), after)
+
+    def store(t, a, b, after=()):
+        ends.append(op("s", lambda: Y.dma_start(T.y[:, t * S + 16 * a:t * S + 16 * b], xc(t, a, b)), reads=xr(t, a, b), dma=True, after=after))
+
+    def hash16(bank, band, src, base, a, b, reads):
+        def fn():
+            ins = None
+            for p in range(16):
+                ins = P.matmul(T[bank][:, 0:b - a], T[band][:, 15 - p:143 - p], src[:, base + 16 * a + p:base + 16 * b:16], p == 0, p == 15)
+            return ins
+        return op("p", fn, reads=list(reads) + [band], writes=[bank])
+
+    load("a", T.hwb[:, 0:3], T.hw[:, 0:3], ["hw"])
+    for k, (a, b, _c, _s) in enumerate(tabp):
+        if k == CFG["res0_at"]:
+            load("s", xc(0, 0, NC), T.res[:, 0:S], xr(0, 0, NC))
+        load("s", T.tb[:, 64 * a:64 * b], T.tab[:, 64 * a:64 * b], rg("tb", a, b))
+    early = CFG["early0"] if rank == 0 else M - 1
+    for t in range(1, early + 1):
+        load_res(t)
+
+    op("g", lambda: g.iota(T.i8[:, 0:8], [[-16, 8]], 0, 1), writes=["i8"])
+    op("g", lambda: g.iota(T.p4i[:, 0:1], [[0, 1]], 0, 4), writes=["p4i"])
+    for a, b, _c, _s in tabp:
+        op("g", lambda a=a, b=b: g.iota(T.jc0[:, a:b], [[64, b - a]], 0, 0), writes=rg("jc0", a, b))
+    for a, b, _e in pieces:
+        op("g", lambda a=a, b=b: g.iota(T.jc1[:, a:b], [[64, b - a]], 0, 0), writes=rg("jc1", a, b))
+    bands = ([("Vb", 1)] if up is not None else []) + [("Wb", 2), ("Ub", 0)]
+    for nm, _k in bands:
+        op("v", lambda nm=nm: V.memset(T[nm][:, :], 0.0), writes=[nm])
+    op("v", lambda: V.tensor_scalar(T.i8[:, 0:8], T.i8[:, 0:8], 4, None, ALU.arith_shift_right), reads=["i8"], writes=["i8"])
+    op("v", lambda: V.tensor_scalar(T.p4i[:, 0:1], T.p4i[:, 0:1], 63, None, ALU.bitwise_and), reads=["p4i"], writes=["p4i"])
+    op("v", lambda: V.tensor_copy(T.p4f[:, 0:1], T.p4i[:, 0:1]), reads=["p4i"], writes=["p4f"])
+    for nm, k in bands:
+        op("v", lambda nm=nm, k=k: V.tensor_scalar(T[nm][:, 15:128:16], T.i8[:, 0:8], 0.0, T.hwb[:, k:k + 1], ALU.is_equal, ALU.mult),
+           reads=["i8", "hw"], writes=[nm])
+
+    if up is not None:
+        rid, pid, _se = topo.addr(up)
+        umask, ucnt = topo.mask(core, up), len(topo.engines(core, up))
+
+    def send(out, in_, reads, rsem, lsem):
+        return op("g", lambda: g.remote_dma(out, in_, T.sem[rsem], T.sem[lsem], pid, rid, umask), reads=reads)
+
+    if up is not None:
+        k = send(T.Vin[:, :], T.Vb[:, :], ["Vb"], "vin", "sent0")
+        ends.append(ext("sent0", ucnt, kn=ops[k]["kn"]))
+    if down is not None:
+        dcnt = len(topo.engines(down, core))
+        ext("vin", dcnt, writes=["Vin"])
+        for t in range(1, M):
+            for c, (a, b) in enumerate(ch):
+                ext("z%d_%d" % (t, c), dcnt, writes=rg("Z%d" % t, a, b))
+
+    def wops(bank, jc, a, b):
+        op("v", lambda: V.tensor_copy(T.wa[:, a:b], T[bank][:, 0:b - a]), writes=[bank] + rg("wa", a, b))
+        op("v", lambda: V.tensor_scalar(T.wa[:, a:b], T.wa[:, a:b], 3, None, ALU.bitwise_and), writes=rg("wa", a, b))
+        op("v", lambda: V.tensor_tensor(T.wa[:, a:b], T.wa[:, a:b], T[jc][:, a:b], ALU.add), reads=rg(jc, a, b), writes=rg("wa", a, b))
+        op("v", lambda: V.tensor_scalar(T.wo[:, a:b], T.wa[:, a:b], T.p4f[:, 0:1], None, ALU.add),
+           reads=rg("wa", a, b) + ["p4f"], writes=rg("wo", a, b))
+
+    def widen(t, a, b):
+        op("a", lambda: A.activation(T.xs[:, 16 * a:16 * b], xc(t, a, b), ACT.Identity, bias=LIFT), reads=xr(t, a, b), writes=rg("xs", a, b))
+
+    def scatter(e, t, a, b):
+        win = T.tf[:, 64 * a:64 * b]
+        if e == "v":
+            op("v", lambda: V.tensor_copy(win.indirect(T.wo[:, a:b]), xc(t, a, b)), reads=xr(t, a, b) + rg("wo", a, b), writes=rg("T", a, b))
+        else:
+            op("a", lambda: A.activation(win.indirect(T.wo[:, a:b]), T.xs[:, 16 * a:16 * b], ACT.Silu),
+               reads=rg("xs", a, b) + rg("wo", a, b), writes=rg("T", a, b))
+
+    def uevac(bank, t, a, b):
+        o = (t % 2) * NC
+        op("a", lambda: A.activation(T.us[:, o + a:o + b], T[bank][:, 0:b - a], ACT.Identity), writes=[bank] + rg("us%d" % (t % 2), a, b))
+
+    def hops(t, a, b, bank, direct=False):
+        o, uk = ((t - 1) % 2) * NC, "us%d" % ((t - 1) % 2)
+        if direct:
+            op("v", lambda: V.tensor_copy(T.ha[:, a:b], T[bank][:, 0:b - a]), writes=[bank] + rg("ha", a, b))
+        elif bank == "vl":
+            op("v", lambda: V.tensor_tensor(T.ha[:, a:b], T.vl[:, (t - 1) * NC + a:(t - 1) * NC + b], T.us[:, o + a:o + b], ALU.add),
+               reads=rg(uk, a, b) + rg("Z%d" % t, a, b), writes=rg("ha", a, b))
+        elif bank is None:
+            op("v", lambda: V.tensor_copy(T.ha[:, a:b], T.us[:, o + a:o + b]), reads=rg(uk, a, b), writes=rg("ha", a, b))
+        else:
+            op("v", lambda: V.tensor_tensor(T.ha[:, a:b], T[bank][:, 0:b - a], T.us[:, o + a:o + b], ALU.add),
+               reads=rg(uk, a, b), writes=[bank] + rg("ha", a, b))
+        op("v", lambda: V.tensor_scalar(T.ha[:, a:b], T.ha[:, a:b], W - 1, None, ALU.bitwise_and), writes=rg("ha", a, b))
+        op("v", lambda: V.tensor_copy(T.ho[:, a:b], T.ha[:, a:b]), reads=rg("ha", a, b), writes=rg("ho", a, b))
+
+    def convert(e, a, b):
+        if e == "a":
+            op("a", lambda: A.activation(T.tf[:, 64 * a:64 * b], T.tb[:, 64 * a:64 * b], ACT.Silu, bias=LIFT), reads=rg("tb", a, b), writes=rg("T", a, b))
+        else:
+            op("v", lambda: V.tensor_copy(T.tf[:, 64 * a:64 * b], T.tb[:, 64 * a:64 * b]), reads=rg("tb", a, b), writes=rg("T", a, b))
+
+    for a, b, ce, se in tabp[:CFG["res0_at"]]:
+        convert(ce, a, b)
+    hash16("pw0", "Wb", T.R, 0, 0, NC, xr(0, 0, NC))
+    hash16("pu0", "Ub", T.R, 0, 0, NC, xr(0, 0, NC))
+    wops("pw0", "jc0", 0, NC)
+    for k, (a, b, ce, se) in enumerate(tabp):
+        if k >= CFG["res0_at"]:
+            convert(ce, a, b)
+        if se == "a":
+            widen(0, a, b)
+        scatter(se, 0, a, b)
+        if k == 0:
+            if rank == 0:
+                hops(1, 0, NC, "pu0", True)
+            else:
+                uevac("pu0", 0, 0, NC)
+    late_y = rank < n - 2
+    if not late_y:
+        store(0, 0, NC, after=[len(ops) - 1])
+
+    nv = [0]
+    pend = []
+
+    def widen_done(t, lo, hi):
+        runs = []
+        for a, b, e in pieces:
+            a, b = max(a, lo), min(b, hi)
+            if e == "a" and a < b:
+                if runs and runs[-1][1] == a:
+                    runs[-1][1] = b
+                else:
+                    runs.append([a, b])
+        for a, b in runs:
+            widen(t, a, b)
+
+    def decode(t, a, b):
+        win = T.tf[:, 0:W].indirect(T.ho[:, a:b])
+        cols = slice(16 * a, 16 * b)
+        op("v", lambda: V.tensor_tensor(T.s32[:, cols], win, xc(t, a, b), ALU.add),
+           reads=rg("T", 0, NC) + rg("ho", a, b) + xr(t, a, b), writes=rg("s", a, b))
+        op("v", lambda: V.tensor_scalar(T.s32[:, cols], T.s32[:, cols], 255, None, ALU.bitwise_and), writes=rg("s", a, b))
+        op("v", lambda: V.tensor_copy(xc(t, a, b), T.s32[:, cols]), reads=rg("s", a, b), writes=xr(t, a, b))
+
+    def vhash(t, c):
+        if down is None:
+            return None
+        if c in far_down:
+            return "vl"
+        a, b = ch[c]
+        bank = "pv%d" % (nv[0] % 2)
+        nv[0] += 1
+        hash16(bank, "Vin", T.Z, (t - 1) * S, a, b, rg("Z%d" % t, a, b))
+        return bank
+
+    def send_v(t, c):
+        a, b = ch[c]
+        bank, o = "px%d" % (c % 2), (t - 1) * NC
+        hash16(bank, "Vb", T.R, t * S, a, b, xr(t, a, b))
+        op("a", lambda: A.activation(T.vo[:, o + a:o + b], T[bank][:, 0:b - a], ACT.Identity), writes=[bank] + rg("vo%d" % t, a, b))
+        return send(T.vl[:, o + a:o + b], T.vo[:, o + a:o + b], rg("vo%d" % t, a, b), "z%d_%d" % (t, c), "sent%d" % t)
+
+    for t in range(1, M):
+        more = t < M - 1
+        w_done = u_done = wo_done = False
+        late = CFG["w1_late"]
+        ks = None
+        banks = {}
+        for c, (a, b) in enumerate(ch):
+            lastc = c == len(ch) - 1
+            if c not in banks:
+                banks[c] = vhash(t, c)
+            if c == 0:
+                for f in pend:
+                    f()
+                del pend[:]
+            if more and w_done and not wo_done and not late:
+                wops("pw0", "jc1", 0, w1)
+                wo_done = True
+            if more and not w_done and a >= w1:
+                hash16("pw0", "Wb", T.R, t * S, 0, w1, xr(t, 0, w1))
+                w_done = True
+                if lastc and not late:
+                    wops("pw0", "jc1", 0, w1)
+                    wo_done = True
+            if more and not u_done and a >= u1:
+                hash16("pu0", "Ub", T.R, t * S, 0, u1, xr(t, 0, u1))
+                uevac("pu0", t, 0, u1)
+                u_done = True
+            if not (rank == 0 and t == 1):
+                hops(t, a, b, banks[c])
+            decode(t, a, b)
+            if c in far_up:
+                if not lastc:
+                    banks[c + 1] = vhash(t, c + 1)
+                ks = send_v(t, c)
+            elif up is not None:
+                ks = send(T.Z[:, (t - 1) * S + 16 * a:(t - 1) * S + 16 * b], xc(t, a, b), xr(t, a, b), "z%d_%d" % (t, c), "sent%d" % t)
+            if more and not lastc:
+                widen_done(t, a, b)
+            if not more and up is None:
+                store(t, a, b)
+        left = []
+        if up is not None:
+            left = [ext("sent%d" % t, ucnt * len(ch), kn=ops[ks]["kn"])]
+            ends.extend(left)
+        if more:
+            hash16("pw1", "Wb", T.R, t * S, w1, NC, xr(t, w1, NC))
+            if not wo_done:
+                wops("pw0", "jc1", 0, w1)
+            for a, b, e in pieces:
+                if b <= w1:
+                    scatter(e, t, a, b)
+            wops("pw1", "jc1", w1, NC)
+            widen_done(t, ch[-1][0], NC)
+            for a, b, e in pieces:
+                if b > w1:
+                    scatter(e, t, a, b)
+
+            def rest(t=t):
+                hash16("pu1", "Ub", T.R, t * S, u1, NC, xr(t, u1, NC))
+                uevac("pu1", t, u1, NC)
+            pend.append(rest)
+            if t + 2 < M and t + 2 > early:
+                load_res(t + 2, after=left)
+            if not late_y:
+                store(t, 0, NC, after=left)
+        elif up is not None:
+            if late_y:
+                for tt in range(M - 1):
+                    store(tt, 0, NC, after=left)
+            store(t, 0, NC, after=left)
+    op("s", None, after=ends)
+    emit(g, T, ops)

@@ -1,55 +1,62 @@
+from concourse.bass import DstId, RemoteDMATransfer
 from concourse.mybir import AluOpType as ALU, ActivationFunctionType as ACT
 
 S, M, W, NC = 1024, 5, 4096, 64
-LIFT = 256.25
+LIFT = 256.0
 
 CFG = {
     "chunks": [0, 16, 32, 48, 64],
-    "w1": 32,
-    "u1": 48,
-    "w1_late": False,
-    "pieces": [(0, 24, "a"), (24, 32, "v"), (32, 52, "a"), (52, 64, "v")],
-    "tab": [(0, 8, "a", "v"), (8, 24, "a", "v"), (24, 40, "a", "v"), (40, 52, "a", "a"), (52, 64, "v", "v")],
+    "w1": 48,
+    "wops_at": 3,
+    "pieces": [(0, 20, "a", 1), (20, 32, "a", 2), (32, 48, "v", 1), (48, 64, "v", 2)],
+    "end": ["a0", "sum", "w", "xs", "x", "v1", "a1", "u", "v", "wo", "us", "a2", "v2"],
+    "tab": [(0, 8, "a", "v"), (8, 24, "a", "v"), (24, 40, "a", "v"), (40, 52, "a", "v"), (52, 60, "a", "a"), (60, 64, "v", "v")],
     "res0_at": 1,
     "early0": 2,
-    "far_v": (0, 2),
 }
 MAXC = 8
 
 SCRATCH = {
     "R": ("sbuf", [128, M * S], "bfloat16"),
-    "Z": ("sbuf", [128, (M - 1) * S], "bfloat16"),
+    "Z": ("sbuf", [128, (M - 1) * S], "float16"),
+    "Vin": ("sbuf", [128, 144], "bfloat16"),
+    "us": ("sbuf", [128, NC], "float32"),
     "tb": ("sbuf", [128, W], "bfloat16"),
     "tf": ("sbuf", [128, W], "float32"),
     "hwb": ("sbuf", [128, 8], "bfloat16"),
     "Ub": ("sbuf", [128, 144], "bfloat16"),
     "Wb": ("sbuf", [128, 144], "bfloat16"),
     "Vb": ("sbuf", [128, 144], "bfloat16"),
-    "Vin": ("sbuf", [128, 144], "bfloat16"),
+    "one": ("sbuf", [128, 128], "bfloat16"),
+    "eye": ("sbuf", [128, 128], "bfloat16"),
+    "neg": ("sbuf", [128, 16], "bfloat16"),
+    "cv": ("sbuf", [128, 4], "float32"),
     "i8": ("sbuf", [128, 8], "int32"),
+    "m8": ("sbuf", [128, 8], "float32"),
     "p4i": ("sbuf", [128, 4], "int32"),
     "p4f": ("sbuf", [128, 4], "float32"),
     "jc0": ("sbuf", [128, NC], "int32"),
     "jc1": ("sbuf", [128, NC], "int32"),
-    "s32": ("sbuf", [128, S], "int32"),
+    "jf0": ("sbuf", [128, NC], "float32"),
+    "jf1": ("sbuf", [128, NC], "float32"),
+    "s16": ("sbuf", [128, M * S], "float16"),
+    "k16": ("sbuf", [128, M * S], "float16"),
     "xs": ("sbuf", [128, S], "float32"),
-    "us": ("sbuf", [128, 2 * NC], "float32"),
-    "vo": ("sbuf", [128, (M - 1) * NC], "float32"),
-    "vl": ("sbuf", [128, (M - 1) * NC], "float32"),
     "ha": ("sbuf", [128, NC], "int32"),
     "ho": ("sbuf", [128, NC], "uint16"),
     "wa": ("sbuf", [128, NC], "int32"),
+    "wf": ("sbuf", [128, NC], "float32"),
     "wo": ("sbuf", [128, NC], "uint16"),
     "pv0": ("psum", [128, 512], "float32"),
     "pv1": ("psum", [128, 512], "float32"),
     "pw0": ("psum", [128, 512], "float32"),
     "pw1": ("psum", [128, 512], "float32"),
-    "pu0": ("psum", [128, 512], "float32"),
-    "pu1": ("psum", [128, 512], "float32"),
+    "pu": ("psum", [128, 512], "float32"),
     "px0": ("psum", [128, 512], "float32"),
     "px1": ("psum", [128, 512], "float32"),
+    "px2": ("psum", [128, 512], "float32"),
 }
-POOL = {"d": 34, "v": 16, "a": 22, "p": 22, "g": 12}
+POOL = {"d": 34, "v": 18, "a": 22, "p": 22, "g": 14}
 SEMAPHORES = ([k + str(i) for k in POOL for i in range(POOL[k])]
               + ["z%d_%d" % (t, c) for t in range(1, M) for c in range(MAXC)] + ["vin"] + ["sent%d" % t for t in range(M)])
 
@@ -94,13 +101,11 @@ def rank_program(g, core, T, topo):
     up = T.cores[rank + 1] if rank + 1 < n else None
     down = T.cores[rank - 1] if rank > 0 else None
     ch = list(zip(CFG["chunks"], CFG["chunks"][1:]))
-    w1, u1, pieces, tabp = CFG["w1"], CFG["u1"], CFG["pieces"], CFG["tab"]
-    far_up = CFG["far_v"] if up is not None and topo.chip(up) != topo.chip(core) else ()
-    far_down = CFG["far_v"] if down is not None and topo.chip(down) != topo.chip(core) else ()
+    w1, pieces, tabp = CFG["w1"], CFG["pieces"], CFG["tab"]
 
     ops, known, writer, readers = [], {}, {}, {}
 
-    def op(q, fn, reads=(), writes=(), dma=False, after=()):
+    def op(q, fn, reads=(), writes=(), dma=False, after=(), group=None):
         k = len(ops)
         deps = set(after)
         for r in reads:
@@ -110,6 +115,7 @@ def rank_program(g, core, T, topo):
             if r in writer:
                 deps.add(writer[r])
             deps.update(readers.get(r, ()))
+        deps.discard(group)
         kn, waits = known.get(q, 0), []
         for d in sorted(deps, reverse=True):
             if not kn >> d & 1:
@@ -139,8 +145,17 @@ def rank_program(g, core, T, topo):
     def xr(t, a, b):
         return rg("R%d" % t, a, b)
 
+    def sr(t, a, b):
+        return rg("s%d" % t, a, b)
+
+    def kr(t, a, b):
+        return rg("k%d" % t, a, b)
+
+    def cols(buf, t, a, b):
+        return buf[:, t * S + 16 * a:t * S + 16 * b]
+
     def xc(t, a, b):
-        return T.R[:, t * S + 16 * a:t * S + 16 * b]
+        return cols(T.R, t, a, b)
 
     def load(q, out, in_, writes, after=()):
         e = A if q == "a" else Y
@@ -149,10 +164,10 @@ def rank_program(g, core, T, topo):
     def load_res(t, after=()):
         cut = [0, ch[0][1], NC] if t == 1 else [0, NC]
         for a, b in zip(cut, cut[1:]):
-            load("s", xc(t, a, b), T.res[:, t * S + 16 * a:t * S + 16 * b], xr(t, a, b), after)
+            load("s", xc(t, a, b), cols(T.res, t, a, b), xr(t, a, b), after)
 
     def store(t, a, b, after=()):
-        ends.append(op("s", lambda: Y.dma_start(T.y[:, t * S + 16 * a:t * S + 16 * b], xc(t, a, b)), reads=xr(t, a, b), dma=True, after=after))
+        ends.append(op("s", lambda: Y.dma_start(cols(T.y, t, a, b), xc(t, a, b)), reads=xr(t, a, b), dma=True, after=after))
 
     def hash16(bank, band, src, base, a, b, reads):
         def fn():
@@ -172,30 +187,32 @@ def rank_program(g, core, T, topo):
         load_res(t)
 
     op("g", lambda: g.iota(T.i8[:, 0:8], [[-16, 8]], 0, 1), writes=["i8"])
-    op("g", lambda: g.iota(T.p4i[:, 0:1], [[0, 1]], 0, 4), writes=["p4i"])
+    op("g", lambda: g.iota(T.p4i[:, 0:1], [[0, 1]], 0, 1), writes=["p4i"])
     for a, b, _c, _s in tabp:
-        op("g", lambda a=a, b=b: g.iota(T.jc0[:, a:b], [[64, b - a]], 0, 0), writes=rg("jc0", a, b))
-    for a, b, _e in pieces:
-        op("g", lambda a=a, b=b: g.iota(T.jc1[:, a:b], [[64, b - a]], 0, 0), writes=rg("jc1", a, b))
-    bands = ([("Vb", 1)] if up is not None else []) + [("Wb", 2), ("Ub", 0)]
+        op("g", lambda a=a, b=b: g.iota(T.jc0[:, a:b], [[16, b - a]], 0, 0), writes=rg("jc0", a, b))
+    bands = [("Wb", 2), ("Ub", 0)] + ([("Vb", 1)] if up is not None else [])
     for nm, _k in bands:
         op("v", lambda nm=nm: V.memset(T[nm][:, :], 0.0), writes=[nm])
+    op("v", lambda: V.memset(T.one[:, :], 1.0), writes=["one"])
+    if down is not None:
+        op("v", lambda: V.memset(T.neg[:, :], -LIFT), writes=["neg"])
     op("v", lambda: V.tensor_scalar(T.i8[:, 0:8], T.i8[:, 0:8], 4, None, ALU.arith_shift_right), reads=["i8"], writes=["i8"])
-    op("v", lambda: V.tensor_scalar(T.p4i[:, 0:1], T.p4i[:, 0:1], 63, None, ALU.bitwise_and), reads=["p4i"], writes=["p4i"])
-    op("v", lambda: V.tensor_copy(T.p4f[:, 0:1], T.p4i[:, 0:1]), reads=["p4i"], writes=["p4f"])
+    op("v", lambda: V.tensor_scalar(T.p4i[:, 0:1], T.p4i[:, 0:1], 15, None, ALU.bitwise_and), reads=["p4i"], writes=["p4i"])
+    op("v", lambda: V.tensor_scalar(T.m8[:, 0:8], T.i8[:, 0:8], 0.0, None, ALU.is_equal), reads=["i8"], writes=["m8"])
+    op("v", lambda: V.tensor_scalar(T.p4f[:, 0:1], T.p4i[:, 0:1], 0.375, None, ALU.add), reads=["p4i"], writes=["p4f"])
+    op("v", lambda: V.tensor_scalar(T.jf0[:, :], T.jc0[:, :], T.p4f[:, 0:1], None, ALU.add), reads=rg("jc0", 0, NC) + ["p4f"], writes=["jf0"])
     for nm, k in bands:
-        op("v", lambda nm=nm, k=k: V.tensor_scalar(T[nm][:, 15:128:16], T.i8[:, 0:8], 0.0, T.hwb[:, k:k + 1], ALU.is_equal, ALU.mult),
-           reads=["i8", "hw"], writes=[nm])
+        op("v", lambda nm=nm, k=k: V.tensor_scalar(T[nm][:, 15:128:16], T.m8[:, 0:8], T.hwb[:, k:k + 1], 0.25 if nm == "Wb" else 1.0, ALU.mult, ALU.mult),
+           reads=["m8", "hw"], writes=[nm])
+    for a, b, _e, _s in pieces:
+        op("g", lambda a=a, b=b: g.iota(T.jc1[:, a:b], [[16, b - a]], 0, 0), writes=rg("jc1", a, b))
+    op("g", lambda: g.affine_select(T.eye[:, :], T.one[:, :], [[-1, 128]], ALU.is_equal, 0.0, 0, 1), reads=["one"], writes=["eye"])
+    op("v", lambda: V.tensor_scalar(T.jf1[:, :], T.jc1[:, :], T.p4f[:, 0:1], None, ALU.add), reads=rg("jc1", 0, NC) + ["p4f"], writes=["jf1"])
 
     if up is not None:
         rid, pid, _se = topo.addr(up)
         umask, ucnt = topo.mask(core, up), len(topo.engines(core, up))
-
-    def send(out, in_, reads, rsem, lsem):
-        return op("g", lambda: g.remote_dma(out, in_, T.sem[rsem], T.sem[lsem], pid, rid, umask), reads=reads)
-
-    if up is not None:
-        k = send(T.Vin[:, :], T.Vb[:, :], ["Vb"], "vin", "sent0")
+        k = op("g", lambda: g.remote_dma(T.Vin[:, :], T.Vb[:, :], T.sem["vin"], T.sem["sent0"], pid, rid, umask), reads=["Vb"])
         ends.append(ext("sent0", ucnt, kn=ops[k]["kn"]))
     if down is not None:
         dcnt = len(topo.engines(down, core))
@@ -204,40 +221,37 @@ def rank_program(g, core, T, topo):
             for c, (a, b) in enumerate(ch):
                 ext("z%d_%d" % (t, c), dcnt, writes=rg("Z%d" % t, a, b))
 
-    def wops(bank, jc, a, b):
-        op("v", lambda: V.tensor_copy(T.wa[:, a:b], T[bank][:, 0:b - a]), writes=[bank] + rg("wa", a, b))
-        op("v", lambda: V.tensor_scalar(T.wa[:, a:b], T.wa[:, a:b], 3, None, ALU.bitwise_and), writes=rg("wa", a, b))
-        op("v", lambda: V.tensor_tensor(T.wa[:, a:b], T.wa[:, a:b], T[jc][:, a:b], ALU.add), reads=rg(jc, a, b), writes=rg("wa", a, b))
-        op("v", lambda: V.tensor_scalar(T.wo[:, a:b], T.wa[:, a:b], T.p4f[:, 0:1], None, ALU.add),
-           reads=rg("wa", a, b) + ["p4f"], writes=rg("wo", a, b))
+    def send(t, c):
+        a, b = ch[c]
+        tr = RemoteDMATransfer(dst_ids=[DstId(rid=rid, pnc=pid)], dma_engine_mask=umask, remote_sem=T.sem["z%d_%d" % (t, c)],
+                               srcs=[cols(T.s16, t, a, b), cols(T.k16, t, a, b)], dsts=[cols(T.Z, t - 1, a, b)], alu_op=1)
+        return op("g", lambda: g.remote_dma_fused([tr], local_sem=T.sem["sent%d" % t]), reads=sr(t, a, b) + kr(t, a, b))
 
-    def widen(t, a, b):
-        op("a", lambda: A.activation(T.xs[:, 16 * a:16 * b], xc(t, a, b), ACT.Identity, bias=LIFT), reads=xr(t, a, b), writes=rg("xs", a, b))
+    def wops(bank, jf, a, b):
+        pb = T[bank][:, 0:b - a]
+        op("v", lambda: V.tensor_tensor(T.wa[:, a:b], pb, T[jf][:, a:b], ALU.subtract), reads=[jf], writes=[bank] + rg("wa", a, b))
+        op("v", lambda: V.tensor_tensor(T.wf[:, a:b], pb, T.wa[:, a:b], ALU.subtract), reads=rg("wa", a, b), writes=[bank] + rg("wf", a, b))
+        op("v", lambda: V.tensor_scalar(T.wo[:, a:b], T.wf[:, a:b], 4.0, None, ALU.mult), reads=rg("wf", a, b), writes=rg("wo", a, b))
 
     def scatter(e, t, a, b):
         win = T.tf[:, 64 * a:64 * b]
-        if e == "v":
-            op("v", lambda: V.tensor_copy(win.indirect(T.wo[:, a:b]), xc(t, a, b)), reads=xr(t, a, b) + rg("wo", a, b), writes=rg("T", a, b))
-        else:
-            op("a", lambda: A.activation(win.indirect(T.wo[:, a:b]), T.xs[:, 16 * a:16 * b], ACT.Silu),
+        if e == "a":
+            op("a", lambda: A.activation(win.indirect(T.wo[:, a:b]), cols(T.xs, 0, a, b), ACT.Silu),
                reads=rg("xs", a, b) + rg("wo", a, b), writes=rg("T", a, b))
-
-    def uevac(bank, t, a, b):
-        o = (t % 2) * NC
-        op("a", lambda: A.activation(T.us[:, o + a:o + b], T[bank][:, 0:b - a], ACT.Identity), writes=[bank] + rg("us%d" % (t % 2), a, b))
-
-    def hops(t, a, b, bank, direct=False):
-        o, uk = ((t - 1) % 2) * NC, "us%d" % ((t - 1) % 2)
-        if direct:
-            op("v", lambda: V.tensor_copy(T.ha[:, a:b], T[bank][:, 0:b - a]), writes=[bank] + rg("ha", a, b))
-        elif bank == "vl":
-            op("v", lambda: V.tensor_tensor(T.ha[:, a:b], T.vl[:, (t - 1) * NC + a:(t - 1) * NC + b], T.us[:, o + a:o + b], ALU.add),
-               reads=rg(uk, a, b) + rg("Z%d" % t, a, b), writes=rg("ha", a, b))
-        elif bank is None:
-            op("v", lambda: V.tensor_copy(T.ha[:, a:b], T.us[:, o + a:o + b]), reads=rg(uk, a, b), writes=rg("ha", a, b))
+        elif t == 0:
+            op("v", lambda: V.tensor_copy(win.indirect(T.wo[:, a:b]), cols(T.s16, 0, a, b)), reads=sr(0, a, b) + rg("wo", a, b), writes=rg("T", a, b))
         else:
-            op("v", lambda: V.tensor_tensor(T.ha[:, a:b], T[bank][:, 0:b - a], T.us[:, o + a:o + b], ALU.add),
-               reads=rg(uk, a, b), writes=[bank] + rg("ha", a, b))
+            op("v", lambda: V.tensor_copy(win.indirect(T.wo[:, a:b]), cols(T.xs, 0, a, b)), reads=rg("xs", a, b) + rg("wo", a, b), writes=rg("T", a, b))
+
+    def uevac():
+        op("a", lambda: A.activation(T.us[:, :], T.pu[:, 0:NC], ACT.Identity, bias=T.cv[:, 0:1]), reads=["cv"], writes=["pu", "us"])
+
+    def hops(t, a, b, bank=None):
+        if down is None:
+            op("v", lambda: V.tensor_copy(T.ha[:, a:b], T.pu[:, a:b]), writes=["pu"] + rg("ha", a, b))
+        else:
+            op("v", lambda: V.tensor_tensor(T.ha[:, a:b], T[bank][:, 0:b - a], T.us[:, a:b], ALU.add),
+               reads=["us"], writes=[bank] + rg("ha", a, b))
         op("v", lambda: V.tensor_scalar(T.ha[:, a:b], T.ha[:, a:b], W - 1, None, ALU.bitwise_and), writes=rg("ha", a, b))
         op("v", lambda: V.tensor_copy(T.ho[:, a:b], T.ha[:, a:b]), reads=rg("ha", a, b), writes=rg("ho", a, b))
 
@@ -245,107 +259,89 @@ def rank_program(g, core, T, topo):
         if e == "a":
             op("a", lambda: A.activation(T.tf[:, 64 * a:64 * b], T.tb[:, 64 * a:64 * b], ACT.Silu, bias=LIFT), reads=rg("tb", a, b), writes=rg("T", a, b))
         else:
-            op("v", lambda: V.tensor_copy(T.tf[:, 64 * a:64 * b], T.tb[:, 64 * a:64 * b]), reads=rg("tb", a, b), writes=rg("T", a, b))
+            op("v", lambda: V.tensor_scalar(T.tf[:, 64 * a:64 * b], T.tb[:, 64 * a:64 * b], LIFT, None, ALU.add), reads=rg("tb", a, b), writes=rg("T", a, b))
 
     for a, b, ce, se in tabp[:CFG["res0_at"]]:
         convert(ce, a, b)
+    op("v", lambda: V.tensor_scalar(cols(T.s16, 0, 0, NC), xc(0, 0, NC), LIFT, None, ALU.add), reads=xr(0, 0, NC), writes=sr(0, 0, NC))
     hash16("pw0", "Wb", T.R, 0, 0, NC, xr(0, 0, NC))
-    hash16("pu0", "Ub", T.R, 0, 0, NC, xr(0, 0, NC))
-    wops("pw0", "jc0", 0, NC)
+    hash16("pu", "Ub", T.R, 0, 0, NC, xr(0, 0, NC))
+    wops("pw0", "jf0", 0, NC)
     for k, (a, b, ce, se) in enumerate(tabp):
         if k >= CFG["res0_at"]:
             convert(ce, a, b)
         if se == "a":
-            widen(0, a, b)
+            op("a", lambda a=a, b=b: A.activation(cols(T.xs, 0, a, b), xc(0, a, b), ACT.Identity, bias=LIFT), reads=xr(0, a, b), writes=rg("xs", a, b))
         scatter(se, 0, a, b)
-        if k == 0:
-            if rank == 0:
-                hops(1, 0, NC, "pu0", True)
-            else:
-                uevac("pu0", 0, 0, NC)
+        if k == 0 and down is None:
+            hops(1, 0, NC)
+    if down is not None:
+        hash16("pw1", "Vin", T.neg, 0, 0, 1, ["neg"])
+        op("a", lambda: A.activation(T.cv[:, 0:1], T.pw1[:, 0:1], ACT.Identity), writes=["pw1", "cv"])
+        uevac()
     late_y = rank < n - 2
     if not late_y:
         store(0, 0, NC, after=[len(ops) - 1])
 
-    nv = [0]
-    pend = []
-
-    def widen_done(t, lo, hi):
-        runs = []
-        for a, b, e in pieces:
-            a, b = max(a, lo), min(b, hi)
-            if e == "a" and a < b:
-                if runs and runs[-1][1] == a:
-                    runs[-1][1] = b
-                else:
-                    runs.append([a, b])
-        for a, b in runs:
-            widen(t, a, b)
-
-    def decode(t, a, b):
+    def gather(t, a, b):
         win = T.tf[:, 0:W].indirect(T.ho[:, a:b])
-        cols = slice(16 * a, 16 * b)
-        op("v", lambda: V.tensor_tensor(T.s32[:, cols], win, xc(t, a, b), ALU.add),
-           reads=rg("T", 0, NC) + rg("ho", a, b) + xr(t, a, b), writes=rg("s", a, b))
-        op("v", lambda: V.tensor_scalar(T.s32[:, cols], T.s32[:, cols], 255, None, ALU.bitwise_and), writes=rg("s", a, b))
-        op("v", lambda: V.tensor_copy(xc(t, a, b), T.s32[:, cols]), reads=rg("s", a, b), writes=xr(t, a, b))
+        op("v", lambda: V.tensor_tensor(cols(T.s16, t, a, b), win, xc(t, a, b), ALU.add),
+           reads=rg("T", 0, NC) + rg("ho", a, b) + xr(t, a, b), writes=sr(t, a, b))
+        op("v", lambda: V.tensor_scalar(cols(T.k16, t, a, b), cols(T.s16, t, a, b), LIFT + 256.0, -256.0, ALU.is_ge, ALU.mult),
+           reads=sr(t, a, b), writes=kr(t, a, b))
+
+    def total(t, c):
+        a, b = ch[c]
+        bank = "px%d" % (c % 3)
+        pb = T[bank][:, 0:16 * (b - a)]
+        k = op("p", lambda: P.matmul(pb, T.eye[:, :], cols(T.s16, t, a, b), True, False), reads=["eye"] + sr(t, a, b), writes=[bank])
+        op("p", lambda: P.matmul(pb, T.eye[:, :], cols(T.k16, t, a, b), False, True), reads=["eye"] + kr(t, a, b), writes=[bank], group=k)
+
+    def lifted(t, c):
+        a, b = ch[c]
+        bank = "px%d" % (c % 3)
+        op("a", lambda: A.activation(cols(T.xs, 0, a, b), T[bank][:, 0:16 * (b - a)], ACT.Identity), writes=[bank] + rg("xs", a, b))
+
+    def sample(t, c):
+        a, b = ch[c]
+        bank = "px%d" % (c % 3)
+        op("a", lambda: A.activation(xc(t, a, b), T[bank][:, 0:16 * (b - a)], ACT.Identity, bias=-LIFT), writes=[bank] + xr(t, a, b))
 
     def vhash(t, c):
         if down is None:
             return None
-        if c in far_down:
-            return "vl"
         a, b = ch[c]
-        bank = "pv%d" % (nv[0] % 2)
-        nv[0] += 1
+        bank = "pv%d" % (c % 2)
         hash16(bank, "Vin", T.Z, (t - 1) * S, a, b, rg("Z%d" % t, a, b))
         return bank
 
-    def send_v(t, c):
-        a, b = ch[c]
-        bank, o = "px%d" % (c % 2), (t - 1) * NC
-        hash16(bank, "Vb", T.R, t * S, a, b, xr(t, a, b))
-        op("a", lambda: A.activation(T.vo[:, o + a:o + b], T[bank][:, 0:b - a], ACT.Identity), writes=[bank] + rg("vo%d" % t, a, b))
-        return send(T.vl[:, o + a:o + b], T.vo[:, o + a:o + b], rg("vo%d" % t, a, b), "z%d_%d" % (t, c), "sent%d" % t)
+    def scatters(t, place, e):
+        for a, b, pe, pl in pieces:
+            if pl == place and pe == e:
+                scatter(e, t, a, b)
 
+    last = len(ch) - 1
+    bank = vhash(1, 0)
     for t in range(1, M):
         more = t < M - 1
-        w_done = u_done = wo_done = False
-        late = CFG["w1_late"]
         ks = None
-        banks = {}
         for c, (a, b) in enumerate(ch):
-            lastc = c == len(ch) - 1
-            if c not in banks:
-                banks[c] = vhash(t, c)
-            if c == 0:
-                for f in pend:
-                    f()
-                del pend[:]
-            if more and w_done and not wo_done and not late:
-                wops("pw0", "jc1", 0, w1)
-                wo_done = True
-            if more and not w_done and a >= w1:
-                hash16("pw0", "Wb", T.R, t * S, 0, w1, xr(t, 0, w1))
-                w_done = True
-                if lastc and not late:
-                    wops("pw0", "jc1", 0, w1)
-                    wo_done = True
-            if more and not u_done and a >= u1:
-                hash16("pu0", "Ub", T.R, t * S, 0, u1, xr(t, 0, u1))
-                uevac("pu0", t, 0, u1)
-                u_done = True
-            if not (rank == 0 and t == 1):
-                hops(t, a, b, banks[c])
-            decode(t, a, b)
-            if c in far_up:
-                if not lastc:
-                    banks[c + 1] = vhash(t, c + 1)
-                ks = send_v(t, c)
-            elif up is not None:
-                ks = send(T.Z[:, (t - 1) * S + 16 * a:(t - 1) * S + 16 * b], xc(t, a, b), xr(t, a, b), "z%d_%d" % (t, c), "sent%d" % t)
-            if more and not lastc:
-                widen_done(t, a, b)
+            if down is not None:
+                hops(t, a, b, bank)
+            if c < last:
+                bank = vhash(t, c + 1)
+            gather(t, a, b)
+            if up is not None:
+                ks = send(t, c)
+            if more and c == CFG["wops_at"]:
+                wops("pw0", "jf1", 0, w1)
+            if c < last or not more:
+                total(t, c)
+                if more and b == w1:
+                    hash16("pw0", "Wb", T.s16, t * S, 0, w1, sr(t, 0, w1))
+                if more:
+                    lifted(t, c)
+                sample(t, c)
             if not more and up is None:
                 store(t, a, b)
         left = []
@@ -353,22 +349,28 @@ def rank_program(g, core, T, topo):
             left = [ext("sent%d" % t, ucnt * len(ch), kn=ops[ks]["kn"])]
             ends.extend(left)
         if more:
-            hash16("pw1", "Wb", T.R, t * S, w1, NC, xr(t, w1, NC))
-            if not wo_done:
-                wops("pw0", "jc1", 0, w1)
-            for a, b, e in pieces:
-                if b <= w1:
-                    scatter(e, t, a, b)
-            wops("pw1", "jc1", w1, NC)
-            widen_done(t, ch[-1][0], NC)
-            for a, b, e in pieces:
-                if b > w1:
-                    scatter(e, t, a, b)
-
-            def rest(t=t):
-                hash16("pu1", "Ub", T.R, t * S, u1, NC, xr(t, u1, NC))
-                uevac("pu1", t, u1, NC)
-            pend.append(rest)
+            for what in CFG["end"]:
+                if what == "sum":
+                    total(t, last)
+                elif what == "xs":
+                    lifted(t, last)
+                elif what == "x":
+                    sample(t, last)
+                elif what == "w":
+                    hash16("pw1", "Wb", T.s16, t * S, w1, NC, sr(t, w1, NC))
+                elif what == "wo":
+                    wops("pw1", "jf1", w1, NC)
+                elif what == "u":
+                    hash16("pu", "Ub", T.R, t * S, 0, NC, xr(t, 0, NC))
+                elif what == "v":
+                    bank = vhash(t + 1, 0)
+                elif what == "us":
+                    if down is not None:
+                        uevac()
+                else:
+                    scatters(t, int(what[1]), what[0])
+            if down is None:
+                hops(t + 1, 0, NC)
             if t + 2 < M and t + 2 > early:
                 load_res(t + 2, after=left)
             if not late_y:

@@ -5,13 +5,21 @@ S, M, W, NC = 1024, 5, 4096, 64
 LIFT = 256.0
 
 CFG = {
-    "chunks": [0, 16, 32, 48, 64],
-    "w1": 48,
-    "wops_at": 3,
-    "pieces": [(0, 20, "a", 1), (20, 32, "a", 2), (32, 48, "v", 1), (48, 64, "v", 2)],
-    "end": ["a0", "sum", "w", "xs", "x", "v1", "a1", "u", "v", "wo", "us", "a2", "v2"],
-    "tab": [(0, 8, "a", "v"), (8, 24, "a", "v"), (24, 40, "a", "v"), (40, 52, "a", "v"), (52, 60, "a", "a"), (60, 64, "v", "v")],
-    "res0_at": 1,
+    "chunks": [0, 22, 44, 64],
+    "w1": 44,
+    "wops_at": 2,
+    "pieces": [(0, 20, "a", 1), (20, 34, "a", 2), (34, 44, "v", 1), (44, 64, "v", 2)],
+    "end": ["sum", "w", "xs", "v1", "a1", "u", "v", "wo", "us", "a2", "v2", "x"],
+    "tab": [(0, 16), (16, 36), (36, 56), (56, 64)],
+    "res0_at": 0,
+    "late": 4,
+    "fin": 10,
+    "mix": True,
+    "gate": "wo",
+    "cv_late": True,
+    "hold": None,
+    "wide0": 56,
+    "early1": 3,
     "early0": 2,
 }
 MAXC = 8
@@ -102,6 +110,7 @@ def rank_program(g, core, T, topo):
     down = T.cores[rank - 1] if rank > 0 else None
     ch = list(zip(CFG["chunks"], CFG["chunks"][1:]))
     w1, pieces, tabp = CFG["w1"], CFG["pieces"], CFG["tab"]
+    last = len(ch) - 1
 
     ops, known, writer, readers = [], {}, {}, {}
 
@@ -161,41 +170,45 @@ def rank_program(g, core, T, topo):
         e = A if q == "a" else Y
         return op(q, lambda: e.dma_start(out, in_), writes=writes, dma=True, after=after)
 
-    def load_res(t, after=()):
-        cut = [0, ch[0][1], NC] if t == 1 else [0, NC]
-        for a, b in zip(cut, cut[1:]):
-            load("s", xc(t, a, b), cols(T.res, t, a, b), xr(t, a, b), after)
+    def load_res(t, a=0, b=NC, after=()):
+        load("s", xc(t, a, b), cols(T.res, t, a, b), xr(t, a, b), after)
 
     def store(t, a, b, after=()):
         ends.append(op("s", lambda: Y.dma_start(cols(T.y, t, a, b), xc(t, a, b)), reads=xr(t, a, b), dma=True, after=after))
 
-    def hash16(bank, band, src, base, a, b, reads):
+    def hash16(bank, band, src, base, a, b, reads, more=()):
+        terms = [(band, src)] + list(more)
+
         def fn():
             ins = None
-            for p in range(16):
-                ins = P.matmul(T[bank][:, 0:b - a], T[band][:, 15 - p:143 - p], src[:, base + 16 * a + p:base + 16 * b:16], p == 0, p == 15)
+            for k, (bd, sc) in enumerate(terms):
+                for p in range(16):
+                    ins = P.matmul(T[bank][:, 0:b - a], T[bd][:, 15 - p:143 - p], sc[:, base + 16 * a + p:base + 16 * b:16],
+                                   k == 0 and p == 0, k == len(terms) - 1 and p == 15)
             return ins
-        return op("p", fn, reads=list(reads) + [band], writes=[bank])
+        return op("p", fn, reads=list(reads) + [bd for bd, _ in terms], writes=[bank])
 
     load("a", T.hwb[:, 0:3], T.hw[:, 0:3], ["hw"])
-    for k, (a, b, _c, _s) in enumerate(tabp):
+    for k, (a, b) in enumerate(tabp):
         if k == CFG["res0_at"]:
             load("s", xc(0, 0, NC), T.res[:, 0:S], xr(0, 0, NC))
         load("s", T.tb[:, 64 * a:64 * b], T.tab[:, 64 * a:64 * b], rg("tb", a, b))
-    early = CFG["early0"] if rank == 0 else M - 1
-    for t in range(1, early + 1):
-        load_res(t)
+    first = ch[0][1]
+    todo = [(t, a, b) for t in range(1, M) for a, b in ((0, first), (first, NC))]
+    if rank > 0:
+        todo = [(t, 0, NC) for t in range(1, M)]
+    for k in range({0: CFG["early0"], 1: CFG["early1"]}.get(rank, M - 1)):
+        load_res(*todo.pop(0), after=[writer[("tb", tabp[CFG["hold"]][0])]] if k and CFG["hold"] is not None else [])
 
     op("g", lambda: g.iota(T.i8[:, 0:8], [[-16, 8]], 0, 1), writes=["i8"])
     op("g", lambda: g.iota(T.p4i[:, 0:1], [[0, 1]], 0, 1), writes=["p4i"])
-    for a, b, _c, _s in tabp:
+    for a, b in tabp:
         op("g", lambda a=a, b=b: g.iota(T.jc0[:, a:b], [[16, b - a]], 0, 0), writes=rg("jc0", a, b))
     bands = [("Wb", 2), ("Ub", 0)] + ([("Vb", 1)] if up is not None else [])
     for nm, _k in bands:
         op("v", lambda nm=nm: V.memset(T[nm][:, :], 0.0), writes=[nm])
     op("v", lambda: V.memset(T.one[:, :], 1.0), writes=["one"])
-    if down is not None:
-        op("v", lambda: V.memset(T.neg[:, :], -LIFT), writes=["neg"])
+    op("v", lambda: V.memset(T.neg[:, :], -LIFT), writes=["neg"])
     op("v", lambda: V.tensor_scalar(T.i8[:, 0:8], T.i8[:, 0:8], 4, None, ALU.arith_shift_right), reads=["i8"], writes=["i8"])
     op("v", lambda: V.tensor_scalar(T.p4i[:, 0:1], T.p4i[:, 0:1], 15, None, ALU.bitwise_and), reads=["p4i"], writes=["p4i"])
     op("v", lambda: V.tensor_scalar(T.m8[:, 0:8], T.i8[:, 0:8], 0.0, None, ALU.is_equal), reads=["i8"], writes=["m8"])
@@ -227,67 +240,85 @@ def rank_program(g, core, T, topo):
                                srcs=[cols(T.s16, t, a, b), cols(T.k16, t, a, b)], dsts=[cols(T.Z, t - 1, a, b)], alu_op=1)
         return op("g", lambda: g.remote_dma_fused([tr], local_sem=T.sem["sent%d" % t]), reads=sr(t, a, b) + kr(t, a, b))
 
-    def wops(bank, jf, a, b):
+    def wops(bank, jf, a, b, calls=(0, 1, 2)):
         pb = T[bank][:, 0:b - a]
-        op("v", lambda: V.tensor_tensor(T.wa[:, a:b], pb, T[jf][:, a:b], ALU.subtract), reads=[jf], writes=[bank] + rg("wa", a, b))
-        op("v", lambda: V.tensor_tensor(T.wf[:, a:b], pb, T.wa[:, a:b], ALU.subtract), reads=rg("wa", a, b), writes=[bank] + rg("wf", a, b))
-        op("v", lambda: V.tensor_scalar(T.wo[:, a:b], T.wf[:, a:b], 4.0, None, ALU.mult), reads=rg("wf", a, b), writes=rg("wo", a, b))
+        if 0 in calls:
+            op("v", lambda: V.tensor_tensor(T.wa[:, a:b], pb, T[jf][:, a:b], ALU.subtract), reads=[jf], writes=[bank] + rg("wa", a, b))
+        if 1 in calls:
+            op("v", lambda: V.tensor_tensor(T.wf[:, a:b], pb, T.wa[:, a:b], ALU.subtract), reads=rg("wa", a, b), writes=[bank] + rg("wf", a, b))
+        if 2 in calls:
+            op("v", lambda: V.tensor_scalar(T.wo[:, a:b], T.wf[:, a:b], 4.0, None, ALU.mult), reads=rg("wf", a, b), writes=rg("wo", a, b))
 
     def scatter(e, t, a, b):
         win = T.tf[:, 64 * a:64 * b]
         if e == "a":
             op("a", lambda: A.activation(win.indirect(T.wo[:, a:b]), cols(T.xs, 0, a, b), ACT.Silu),
                reads=rg("xs", a, b) + rg("wo", a, b), writes=rg("T", a, b))
-        elif t == 0:
-            op("v", lambda: V.tensor_copy(win.indirect(T.wo[:, a:b]), cols(T.s16, 0, a, b)), reads=sr(0, a, b) + rg("wo", a, b), writes=rg("T", a, b))
         else:
             op("v", lambda: V.tensor_copy(win.indirect(T.wo[:, a:b]), cols(T.xs, 0, a, b)), reads=rg("xs", a, b) + rg("wo", a, b), writes=rg("T", a, b))
 
-    def uevac():
-        op("a", lambda: A.activation(T.us[:, :], T.pu[:, 0:NC], ACT.Identity, bias=T.cv[:, 0:1]), reads=["cv"], writes=["pu", "us"])
+    def uevac(t):
+        if t == 0:
+            op("a", lambda: A.activation(T.us[:, :], T.pu[:, 0:NC], ACT.Identity), writes=["pu"] + rg("us", 0, NC))
+        else:
+            cv = T.cv[:, 0:1] if t == 1 or "ux" in CFG["end"] else T.cv[:, 1:2]
+            op("a", lambda: A.activation(T.us[:, :], T.pu[:, 0:NC], ACT.Identity, bias=cv), reads=["cv"], writes=["pu"] + rg("us", 0, NC))
 
-    def hops(t, a, b, bank=None):
-        if down is None:
+    def hops(t, a, b, bank=None, fill=lambda k: None):
+        if down is None and (t <= 2 or "ux" in CFG["end"]):
             op("v", lambda: V.tensor_copy(T.ha[:, a:b], T.pu[:, a:b]), writes=["pu"] + rg("ha", a, b))
+        elif down is None:
+            op("v", lambda: V.tensor_scalar(T.ha[:, a:b], T.pu[:, a:b], T.cv[:, 1:2], None, ALU.add), reads=["cv"], writes=["pu"] + rg("ha", a, b))
         else:
             op("v", lambda: V.tensor_tensor(T.ha[:, a:b], T[bank][:, 0:b - a], T.us[:, a:b], ALU.add),
-               reads=["us"], writes=[bank] + rg("ha", a, b))
+               reads=rg("us", a, b), writes=[bank] + rg("ha", a, b))
+        fill(0)
         op("v", lambda: V.tensor_scalar(T.ha[:, a:b], T.ha[:, a:b], W - 1, None, ALU.bitwise_and), writes=rg("ha", a, b))
+        fill(1)
         op("v", lambda: V.tensor_copy(T.ho[:, a:b], T.ha[:, a:b]), reads=rg("ha", a, b), writes=rg("ho", a, b))
+        fill(2)
 
-    def convert(e, a, b):
-        if e == "a":
-            op("a", lambda: A.activation(T.tf[:, 64 * a:64 * b], T.tb[:, 64 * a:64 * b], ACT.Silu, bias=LIFT), reads=rg("tb", a, b), writes=rg("T", a, b))
-        else:
-            op("v", lambda: V.tensor_scalar(T.tf[:, 64 * a:64 * b], T.tb[:, 64 * a:64 * b], LIFT, None, ALU.add), reads=rg("tb", a, b), writes=rg("T", a, b))
-
-    for a, b, ce, se in tabp[:CFG["res0_at"]]:
-        convert(ce, a, b)
-    op("v", lambda: V.tensor_scalar(cols(T.s16, 0, 0, NC), xc(0, 0, NC), LIFT, None, ALU.add), reads=xr(0, 0, NC), writes=sr(0, 0, NC))
     hash16("pw0", "Wb", T.R, 0, 0, NC, xr(0, 0, NC))
     hash16("pu", "Ub", T.R, 0, 0, NC, xr(0, 0, NC))
     wops("pw0", "jf0", 0, NC)
-    for k, (a, b, ce, se) in enumerate(tabp):
-        if k >= CFG["res0_at"]:
-            convert(ce, a, b)
-        if se == "a":
-            op("a", lambda a=a, b=b: A.activation(cols(T.xs, 0, a, b), xc(0, a, b), ACT.Identity, bias=LIFT), reads=xr(0, a, b), writes=rg("xs", a, b))
-        scatter(se, 0, a, b)
+    if down is not None:
+        uevac(0)
+    wide = CFG["wide0"] if down is None else NC
+    for k, (a, b) in enumerate(tabp):
+        op("v", lambda a=a, b=b: V.tensor_copy(T.tb[:, 64 * a:64 * b].indirect(T.wo[:, a:b]), xc(0, a, b)),
+           reads=xr(0, a, b) + rg("wo", a, b), writes=rg("tb", a, b))
+        b = max(a, min(b, wide))
+        if a < b:
+            op("a", lambda a=a, b=b: A.activation(T.tf[:, 64 * a:64 * b], T.tb[:, 64 * a:64 * b], ACT.Silu, bias=LIFT), reads=rg("tb", a, b), writes=rg("T", a, b))
         if k == 0 and down is None:
             hops(1, 0, NC)
-    if down is not None:
+    if "ux" not in CFG["end"]:
+        hash16("pw1", "Ub", T.neg, 0, 0, 1, ["neg"])
+        op("a", lambda: A.activation(T.cv[:, 1:2], T.pw1[:, 0:1], ACT.Identity), writes=["pw1", "cv"])
+
+    def lift_v():
         hash16("pw1", "Vin", T.neg, 0, 0, 1, ["neg"])
         op("a", lambda: A.activation(T.cv[:, 0:1], T.pw1[:, 0:1], ACT.Identity), writes=["pw1", "cv"])
-        uevac()
-    late_y = rank < n - 2
+        if "ux" not in CFG["end"]:
+            op("a", lambda: A.activation(T.cv[:, 1:2], T.pw1[:, 0:1], ACT.Identity, bias=T.cv[:, 1:2]), writes=["pw1", "cv"])
+
+    if down is not None and not CFG["cv_late"]:
+        lift_v()
+    late_y = rank < CFG["late"]
     if not late_y:
         store(0, 0, NC, after=[len(ops) - 1])
 
-    def gather(t, a, b):
-        win = T.tf[:, 0:W].indirect(T.ho[:, a:b])
+    def lift(t):
+        return 0.0 if t == 1 else LIFT
+
+    def gather(t, a, b, between=None):
+        tab, name = (T.tb, "tb") if t == 1 else (T.tf, "T")
+        win = tab[:, 0:W].indirect(T.ho[:, a:b])
         op("v", lambda: V.tensor_tensor(cols(T.s16, t, a, b), win, xc(t, a, b), ALU.add),
-           reads=rg("T", 0, NC) + rg("ho", a, b) + xr(t, a, b), writes=sr(t, a, b))
-        op("v", lambda: V.tensor_scalar(cols(T.k16, t, a, b), cols(T.s16, t, a, b), LIFT + 256.0, -256.0, ALU.is_ge, ALU.mult),
+           reads=rg(name, 0, NC) + rg("ho", a, b) + xr(t, a, b), writes=sr(t, a, b))
+        if between:
+            between()
+        op("v", lambda: V.tensor_scalar(cols(T.k16, t, a, b), cols(T.s16, t, a, b), lift(t) + 256.0, -256.0, ALU.is_ge, ALU.mult),
            reads=sr(t, a, b), writes=kr(t, a, b))
 
     def total(t, c):
@@ -300,12 +331,24 @@ def rank_program(g, core, T, topo):
     def lifted(t, c):
         a, b = ch[c]
         bank = "px%d" % (c % 3)
-        op("a", lambda: A.activation(cols(T.xs, 0, a, b), T[bank][:, 0:16 * (b - a)], ACT.Identity), writes=[bank] + rg("xs", a, b))
+        op("a", lambda: A.activation(cols(T.xs, 0, a, b), T[bank][:, 0:16 * (b - a)], ACT.Identity, bias=LIFT - lift(t)),
+           reads=[bank], writes=rg("xs", a, b))
 
     def sample(t, c):
         a, b = ch[c]
         bank = "px%d" % (c % 3)
-        op("a", lambda: A.activation(xc(t, a, b), T[bank][:, 0:16 * (b - a)], ACT.Identity, bias=-LIFT), writes=[bank] + xr(t, a, b))
+        op("a", lambda: A.activation(xc(t, a, b), T[bank][:, 0:16 * (b - a)], ACT.Identity, bias=-lift(t)), reads=[bank], writes=xr(t, a, b))
+
+    def finish(t, a, b):
+        m = a + CFG["fin"]
+        parts = [("pw0", a, m), ("pw1", m, b)]
+        heads = [op("p", lambda n_=n_, lo=lo, hi=hi: P.matmul(T[n_][:, 0:16 * (hi - lo)], T.eye[:, :], cols(T.s16, t, lo, hi), True, False),
+                    reads=["eye"] + sr(t, lo, hi), writes=[n_]) for n_, lo, hi in parts]
+        for k, (n_, lo, hi) in zip(heads, parts):
+            op("p", lambda n_=n_, lo=lo, hi=hi: P.matmul(T[n_][:, 0:16 * (hi - lo)], T.eye[:, :], cols(T.k16, t, lo, hi), False, True),
+               reads=["eye"] + kr(t, lo, hi), writes=[n_], group=k)
+        op("a", lambda: A.activation(xc(t, a, m), T.pw0[:, 0:16 * (m - a)], ACT.Identity, bias=-lift(t)), reads=["pw0"], writes=xr(t, a, m))
+        op("v", lambda: V.tensor_scalar(xc(t, m, b), T.pw1[:, 0:16 * (b - m)], -lift(t), None, ALU.add), reads=["pw1"], writes=xr(t, m, b))
 
     def vhash(t, c):
         if down is None:
@@ -320,22 +363,31 @@ def rank_program(g, core, T, topo):
             if pl == place and pe == e:
                 scatter(e, t, a, b)
 
-    last = len(ch) - 1
     bank = vhash(1, 0)
+    if down is not None and CFG["cv_late"]:
+        lift_v()
     for t in range(1, M):
         more = t < M - 1
         ks = None
         for c, (a, b) in enumerate(ch):
-            if down is not None:
+            weave = more and c == last and w1 < a and down is not None
+            if weave:
+                hops(t, a, b, bank, lambda k: wops("pw0", "jf1", 0, w1, (k,)))
+            elif down is not None:
                 hops(t, a, b, bank)
             if c < last:
                 bank = vhash(t, c + 1)
-            gather(t, a, b)
+            mix = more and c == CFG["wops_at"] and down is not None and CFG["mix"] and not weave
+            gather(t, a, b, (lambda: wops("pw0", "jf1", 0, w1, (0,))) if mix else None)
             if up is not None:
                 ks = send(t, c)
-            if more and c == CFG["wops_at"]:
-                wops("pw0", "jf1", 0, w1)
-            if c < last or not more:
+            if t == 1 and c == last and wide < NC:
+                op("v", lambda: V.tensor_scalar(T.tf[:, 64 * wide:W], T.tb[:, 64 * wide:W], LIFT, None, ALU.add), reads=rg("tb", wide, NC), writes=rg("T", wide, NC))
+            if more and c == CFG["wops_at"] and not weave:
+                wops("pw0", "jf1", 0, w1, (1, 2) if mix else (0, 1, 2))
+            if up is None and c == last and not more:
+                finish(t, a, b)
+            elif c < last or not more:
                 total(t, c)
                 if more and b == w1:
                     hash16("pw0", "Wb", T.s16, t * S, 0, w1, sr(t, 0, w1))
@@ -344,10 +396,6 @@ def rank_program(g, core, T, topo):
                 sample(t, c)
             if not more and up is None:
                 store(t, a, b)
-        left = []
-        if up is not None:
-            left = [ext("sent%d" % t, ucnt * len(ch), kn=ops[ks]["kn"])]
-            ends.extend(left)
         if more:
             for what in CFG["end"]:
                 if what == "sum":
@@ -361,20 +409,45 @@ def rank_program(g, core, T, topo):
                 elif what == "wo":
                     wops("pw1", "jf1", w1, NC)
                 elif what == "u":
+                    hash16("pu", "Ub", T.s16, t * S, 0, NC, sr(t, 0, NC) + kr(t, 0, NC), [("Ub", T.k16)])
+                elif what in ("u0", "us0", "us1") and down is None:
+                    pass
+                elif what == "u1" and down is None:
+                    hash16("pu", "Ub", T.s16, t * S, 0, NC, sr(t, 0, NC) + kr(t, 0, NC), [("Ub", T.k16)])
+                elif what == "u0":
+                    hash16("pu", "Ub", T.R, t * S, 0, first, xr(t, 0, first))
+                elif what == "us0":
+                    op("a", lambda: A.activation(T.us[:, 0:first], T.pu[:, 0:first], ACT.Identity, bias=T.cv[:, 0:1]), reads=["cv"], writes=["pu"] + rg("us", 0, first))
+                elif what == "u1":
+                    hash16("pw0", "Ub", T.s16, t * S, first, NC, sr(t, first, NC) + kr(t, first, NC), [("Ub", T.k16)])
+                elif what == "us1":
+                    op("a", lambda t=t: A.activation(T.us[:, first:NC], T.pw0[:, 0:NC - first], ACT.Identity, bias=T.cv[:, 0:1] if t == 1 else T.cv[:, 1:2]),
+                       reads=["cv"], writes=["pw0"] + rg("us", first, NC))
+                elif what == "ux":
                     hash16("pu", "Ub", T.R, t * S, 0, NC, xr(t, 0, NC))
                 elif what == "v":
                     bank = vhash(t + 1, 0)
                 elif what == "us":
                     if down is not None:
-                        uevac()
+                        uevac(t)
                 else:
                     scatters(t, int(what[1]), what[0])
+                if what == CFG["gate"]:
+                    gate = [len(ops) - 1]
             if down is None:
                 hops(t + 1, 0, NC)
-            if t + 2 < M and t + 2 > early:
-                load_res(t + 2, after=left)
+        left = []
+        if up is not None:
+            left = [ext("sent%d" % t, ucnt * len(ch), kn=ops[ks]["kn"])]
+            ends.extend(left)
+        if more:
+            if CFG["gate"] is None:
+                gate = left
+            for _ in range(2):
+                if todo:
+                    load_res(*todo.pop(0), after=gate)
             if not late_y:
-                store(t, 0, NC, after=left)
+                store(t, 0, NC, after=gate)
         elif up is not None:
             if late_y:
                 for tt in range(M - 1):

@@ -6,23 +6,18 @@ LIFT = 256.0
 
 CFG = {
     "chunks": [0, 22, 44, 64],
-    "w1": 44,
-    "wops_at": 2,
-    "pieces": [(0, 20, "a", 1), (20, 34, "a", 2), (34, 44, "v", 1), (44, 64, "v", 2)],
-    "end": ["sum", "w", "xs", "v1", "a1", "u", "v", "wo", "us", "a2", "v2", "x"],
+    "w1": 22,
+    "pieces": [(0, 10, "a1"), (10, 16, "v1"), (16, 18, "v2"), (18, 20, "v3"), (20, 22, "v4"), (22, 40, "v5"), (40, 42, "v6"),
+               (42, 44, "v7"), (44, 54, "a2"), (54, 64, "a3")],
+    "order": ["hv G1 G2 wa K1 A K2 send B C", "hv sum- xs- x- G1 G2 K1 A K2 send p0 B p1 C p2 sum xs x", "G K send"],
+    "end": "a1 wb sum v1 q0 v2 q1 v3 q2 gate v4 xs u hv a2 us a3 v5 A v6 B v7 C x",
     "tab": [(0, 16), (16, 36), (36, 56), (56, 64)],
-    "res0_at": 0,
     "late": 4,
     "fin": 10,
-    "mix": True,
-    "gate": "wo",
-    "cv_late": True,
-    "hold": None,
     "wide0": 56,
-    "early1": 3,
-    "early0": 2,
+    "early": (2, 3),
 }
-MAXC = 8
+MAXC = 6
 
 SCRATCH = {
     "R": ("sbuf", [128, M * S], "bfloat16"),
@@ -43,8 +38,7 @@ SCRATCH = {
     "m8": ("sbuf", [128, 8], "float32"),
     "p4i": ("sbuf", [128, 4], "int32"),
     "p4f": ("sbuf", [128, 4], "float32"),
-    "jc0": ("sbuf", [128, NC], "int32"),
-    "jc1": ("sbuf", [128, NC], "int32"),
+    "jc": ("sbuf", [128, NC], "int32"),
     "jf0": ("sbuf", [128, NC], "float32"),
     "jf1": ("sbuf", [128, NC], "float32"),
     "s16": ("sbuf", [128, M * S], "float16"),
@@ -64,7 +58,7 @@ SCRATCH = {
     "px1": ("psum", [128, 512], "float32"),
     "px2": ("psum", [128, 512], "float32"),
 }
-POOL = {"d": 34, "v": 18, "a": 22, "p": 22, "g": 14}
+POOL = {"d": 34, "v": 26, "a": 22, "p": 22, "g": 14}
 SEMAPHORES = ([k + str(i) for k in POOL for i in range(POOL[k])]
               + ["z%d_%d" % (t, c) for t in range(1, M) for c in range(MAXC)] + ["vin"] + ["sent%d" % t for t in range(M)])
 
@@ -170,40 +164,39 @@ def rank_program(g, core, T, topo):
         e = A if q == "a" else Y
         return op(q, lambda: e.dma_start(out, in_), writes=writes, dma=True, after=after)
 
-    def load_res(t, a=0, b=NC, after=()):
+    def load_res(t, a, b, after=()):
         load("s", xc(t, a, b), cols(T.res, t, a, b), xr(t, a, b), after)
 
     def store(t, a, b, after=()):
         ends.append(op("s", lambda: Y.dma_start(cols(T.y, t, a, b), xc(t, a, b)), reads=xr(t, a, b), dma=True, after=after))
 
-    def hash16(bank, band, src, base, a, b, reads, more=()):
-        terms = [(band, src)] + list(more)
-
+    def hash16(bank, band, srcs, base, a, b, reads):
         def fn():
             ins = None
-            for k, (bd, sc) in enumerate(terms):
+            for k, src in enumerate(srcs):
                 for p in range(16):
-                    ins = P.matmul(T[bank][:, 0:b - a], T[bd][:, 15 - p:143 - p], sc[:, base + 16 * a + p:base + 16 * b:16],
-                                   k == 0 and p == 0, k == len(terms) - 1 and p == 15)
+                    ins = P.matmul(T[bank][:, 0:b - a], T[band][:, 15 - p:143 - p], src[:, base + 16 * a + p:base + 16 * b:16],
+                                   k == 0 and p == 0, k == len(srcs) - 1 and p == 15)
             return ins
-        return op("p", fn, reads=list(reads) + [bd for bd, _ in terms], writes=[bank])
+        return op("p", fn, reads=list(reads) + [band], writes=[bank])
 
     load("a", T.hwb[:, 0:3], T.hw[:, 0:3], ["hw"])
-    for k, (a, b) in enumerate(tabp):
-        if k == CFG["res0_at"]:
-            load("s", xc(0, 0, NC), T.res[:, 0:S], xr(0, 0, NC))
+    load_res(0, 0, NC)
+    for a, b in tabp:
         load("s", T.tb[:, 64 * a:64 * b], T.tab[:, 64 * a:64 * b], rg("tb", a, b))
-    first = ch[0][1]
-    todo = [(t, a, b) for t in range(1, M) for a, b in ((0, first), (first, NC))]
-    if rank > 0:
-        todo = [(t, 0, NC) for t in range(1, M)]
-    for k in range({0: CFG["early0"], 1: CFG["early1"]}.get(rank, M - 1)):
-        load_res(*todo.pop(0), after=[writer[("tb", tabp[CFG["hold"]][0])]] if k and CFG["hold"] is not None else [])
+    cut = [0, ch[0][1], NC] if down is None else [0, NC]
+    todo = [(t, a, b) for t in range(1, M) for a, b in zip(cut, cut[1:])]
+    for _ in range(CFG["early"][rank] if rank < len(CFG["early"]) else M - 1):
+        load_res(*todo.pop(0))
 
     op("g", lambda: g.iota(T.i8[:, 0:8], [[-16, 8]], 0, 1), writes=["i8"])
     op("g", lambda: g.iota(T.p4i[:, 0:1], [[0, 1]], 0, 1), writes=["p4i"])
-    for a, b in tabp:
-        op("g", lambda a=a, b=b: g.iota(T.jc0[:, a:b], [[16, b - a]], 0, 0), writes=rg("jc0", a, b))
+    op("g", lambda: g.iota(T.jc[:, :], [[16, NC]], 0, 0), writes=["jc"])
+
+    def streams(jf, windows):
+        for a, b in windows:
+            op("v", lambda a=a, b=b: V.tensor_scalar(T[jf][:, a:b], T.jc[:, a:b], T.p4f[:, 0:1], -16.0 * a, ALU.add, ALU.add), reads=["jc", "p4f"], writes=rg(jf, a, b))
+
     bands = [("Wb", 2), ("Ub", 0)] + ([("Vb", 1)] if up is not None else [])
     for nm, _k in bands:
         op("v", lambda nm=nm: V.memset(T[nm][:, :], 0.0), writes=[nm])
@@ -213,14 +206,12 @@ def rank_program(g, core, T, topo):
     op("v", lambda: V.tensor_scalar(T.p4i[:, 0:1], T.p4i[:, 0:1], 15, None, ALU.bitwise_and), reads=["p4i"], writes=["p4i"])
     op("v", lambda: V.tensor_scalar(T.m8[:, 0:8], T.i8[:, 0:8], 0.0, None, ALU.is_equal), reads=["i8"], writes=["m8"])
     op("v", lambda: V.tensor_scalar(T.p4f[:, 0:1], T.p4i[:, 0:1], 0.375, None, ALU.add), reads=["p4i"], writes=["p4f"])
-    op("v", lambda: V.tensor_scalar(T.jf0[:, :], T.jc0[:, :], T.p4f[:, 0:1], None, ALU.add), reads=rg("jc0", 0, NC) + ["p4f"], writes=["jf0"])
+    streams("jf0", tabp)
     for nm, k in bands:
         op("v", lambda nm=nm, k=k: V.tensor_scalar(T[nm][:, 15:128:16], T.m8[:, 0:8], T.hwb[:, k:k + 1], 0.25 if nm == "Wb" else 1.0, ALU.mult, ALU.mult),
            reads=["m8", "hw"], writes=[nm])
-    for a, b, _e, _s in pieces:
-        op("g", lambda a=a, b=b: g.iota(T.jc1[:, a:b], [[16, b - a]], 0, 0), writes=rg("jc1", a, b))
     op("g", lambda: g.affine_select(T.eye[:, :], T.one[:, :], [[-1, 128]], ALU.is_equal, 0.0, 0, 1), reads=["one"], writes=["eye"])
-    op("v", lambda: V.tensor_scalar(T.jf1[:, :], T.jc1[:, :], T.p4f[:, 0:1], None, ALU.add), reads=rg("jc1", 0, NC) + ["p4f"], writes=["jf1"])
+    streams("jf1", [pc[:2] for pc in pieces])
 
     if up is not None:
         rid, pid, _se = topo.addr(up)
@@ -240,214 +231,193 @@ def rank_program(g, core, T, topo):
                                srcs=[cols(T.s16, t, a, b), cols(T.k16, t, a, b)], dsts=[cols(T.Z, t - 1, a, b)], alu_op=1)
         return op("g", lambda: g.remote_dma_fused([tr], local_sem=T.sem["sent%d" % t]), reads=sr(t, a, b) + kr(t, a, b))
 
-    def wops(bank, jf, a, b, calls=(0, 1, 2)):
+    def wop(k, bank, jf, a, b):
         pb = T[bank][:, 0:b - a]
-        if 0 in calls:
-            op("v", lambda: V.tensor_tensor(T.wa[:, a:b], pb, T[jf][:, a:b], ALU.subtract), reads=[jf], writes=[bank] + rg("wa", a, b))
-        if 1 in calls:
+        if k == 0:
+            op("v", lambda: V.tensor_tensor(T.wa[:, a:b], pb, T[jf][:, a:b], ALU.subtract), reads=rg(jf, a, b), writes=[bank] + rg("wa", a, b))
+        elif k == 1:
             op("v", lambda: V.tensor_tensor(T.wf[:, a:b], pb, T.wa[:, a:b], ALU.subtract), reads=rg("wa", a, b), writes=[bank] + rg("wf", a, b))
-        if 2 in calls:
+        else:
             op("v", lambda: V.tensor_scalar(T.wo[:, a:b], T.wf[:, a:b], 4.0, None, ALU.mult), reads=rg("wf", a, b), writes=rg("wo", a, b))
 
-    def scatter(e, t, a, b):
-        win = T.tf[:, 64 * a:64 * b]
-        if e == "a":
-            op("a", lambda: A.activation(win.indirect(T.wo[:, a:b]), cols(T.xs, 0, a, b), ACT.Silu),
-               reads=rg("xs", a, b) + rg("wo", a, b), writes=rg("T", a, b))
-        else:
-            op("v", lambda: V.tensor_copy(win.indirect(T.wo[:, a:b]), cols(T.xs, 0, a, b)), reads=rg("xs", a, b) + rg("wo", a, b), writes=rg("T", a, b))
-
-    def uevac(t):
-        if t == 0:
-            op("a", lambda: A.activation(T.us[:, :], T.pu[:, 0:NC], ACT.Identity), writes=["pu"] + rg("us", 0, NC))
-        else:
-            cv = T.cv[:, 0:1] if t == 1 or "ux" in CFG["end"] else T.cv[:, 1:2]
-            op("a", lambda: A.activation(T.us[:, :], T.pu[:, 0:NC], ACT.Identity, bias=cv), reads=["cv"], writes=["pu"] + rg("us", 0, NC))
-
-    def hops(t, a, b, bank=None, fill=lambda k: None):
-        if down is None and (t <= 2 or "ux" in CFG["end"]):
+    def hop(k, t, c):
+        a, b = ch[c]
+        if down is None:
+            if c > 0:
+                return
+            b = NC
+        if k == 1:
+            op("v", lambda: V.tensor_scalar(T.ha[:, a:b], T.ha[:, a:b], W - 1, None, ALU.bitwise_and), writes=rg("ha", a, b))
+        elif k == 2:
+            op("v", lambda: V.tensor_copy(T.ho[:, a:b], T.ha[:, a:b]), reads=rg("ha", a, b), writes=rg("ho", a, b))
+        elif down is not None:
+            bank = "pv%d" % (c % 2)
+            op("v", lambda: V.tensor_tensor(T.ha[:, a:b], T[bank][:, 0:b - a], T.us[:, a:b], ALU.add), reads=rg("us", a, b), writes=[bank] + rg("ha", a, b))
+        elif t <= 2:
             op("v", lambda: V.tensor_copy(T.ha[:, a:b], T.pu[:, a:b]), writes=["pu"] + rg("ha", a, b))
-        elif down is None:
-            op("v", lambda: V.tensor_scalar(T.ha[:, a:b], T.pu[:, a:b], T.cv[:, 1:2], None, ALU.add), reads=["cv"], writes=["pu"] + rg("ha", a, b))
         else:
-            op("v", lambda: V.tensor_tensor(T.ha[:, a:b], T[bank][:, 0:b - a], T.us[:, a:b], ALU.add),
-               reads=rg("us", a, b), writes=[bank] + rg("ha", a, b))
-        fill(0)
-        op("v", lambda: V.tensor_scalar(T.ha[:, a:b], T.ha[:, a:b], W - 1, None, ALU.bitwise_and), writes=rg("ha", a, b))
-        fill(1)
-        op("v", lambda: V.tensor_copy(T.ho[:, a:b], T.ha[:, a:b]), reads=rg("ha", a, b), writes=rg("ho", a, b))
-        fill(2)
+            op("v", lambda: V.tensor_scalar(T.ha[:, a:b], T.pu[:, a:b], T.cv[:, 1:2], None, ALU.add), reads=["cv"], writes=["pu"] + rg("ha", a, b))
 
-    hash16("pw0", "Wb", T.R, 0, 0, NC, xr(0, 0, NC))
-    hash16("pu", "Ub", T.R, 0, 0, NC, xr(0, 0, NC))
-    wops("pw0", "jf0", 0, NC)
-    if down is not None:
-        uevac(0)
+    def scatter(t, name):
+        for a, b, nm in pieces:
+            if nm == name:
+                out, src = T.tf[:, 64 * a:64 * b].indirect(T.wo[:, a:b]), cols(T.xs, 0, a, b)
+                fn = (lambda out=out, src=src: A.activation(out, src, ACT.Silu)) if nm[0] == "a" else (lambda out=out, src=src: V.tensor_copy(out, src))
+                op(nm[0], fn, reads=rg("xs", a, b) + rg("wo", a, b), writes=rg("T", a, b))
+
+    def uevac(t, bank="pu", a=0, b=NC):
+        if down is not None:
+            bias = 0.0 if t == 0 else T.cv[:, 0:1] if t == 1 else T.cv[:, 1:2]
+            op("a", lambda: A.activation(T.us[:, a:b], T[bank][:, 0:b - a], ACT.Identity, bias=bias), reads=["cv"] if t else [], writes=[bank] + rg("us", a, b))
+
+    def vhash(t, c):
+        if down is not None:
+            a, b = ch[c]
+            hash16("pv%d" % (c % 2), "Vin", [T.Z], (t - 1) * S, a, b, rg("Z%d" % t, a, b))
+
+    hash16("pw0", "Wb", [T.R], 0, 0, NC, xr(0, 0, NC))
+    hash16("pu", "Ub", [T.R], 0, 0, NC, xr(0, 0, NC))
+    for k in range(3):
+        wop(k, "pw0", "jf0", 0, NC)
+    uevac(0)
     wide = CFG["wide0"] if down is None else NC
     for k, (a, b) in enumerate(tabp):
         op("v", lambda a=a, b=b: V.tensor_copy(T.tb[:, 64 * a:64 * b].indirect(T.wo[:, a:b]), xc(0, a, b)),
            reads=xr(0, a, b) + rg("wo", a, b), writes=rg("tb", a, b))
-        b = max(a, min(b, wide))
+        b = min(b, wide)
         if a < b:
             op("a", lambda a=a, b=b: A.activation(T.tf[:, 64 * a:64 * b], T.tb[:, 64 * a:64 * b], ACT.Silu, bias=LIFT), reads=rg("tb", a, b), writes=rg("T", a, b))
-        if k == 0 and down is None:
-            hops(1, 0, NC)
-    if "ux" not in CFG["end"]:
-        hash16("pw1", "Ub", T.neg, 0, 0, 1, ["neg"])
-        op("a", lambda: A.activation(T.cv[:, 1:2], T.pw1[:, 0:1], ACT.Identity), writes=["pw1", "cv"])
-
-    def lift_v():
-        hash16("pw1", "Vin", T.neg, 0, 0, 1, ["neg"])
-        op("a", lambda: A.activation(T.cv[:, 0:1], T.pw1[:, 0:1], ACT.Identity), writes=["pw1", "cv"])
-        if "ux" not in CFG["end"]:
-            op("a", lambda: A.activation(T.cv[:, 1:2], T.pw1[:, 0:1], ACT.Identity, bias=T.cv[:, 1:2]), writes=["pw1", "cv"])
-
-    if down is not None and not CFG["cv_late"]:
-        lift_v()
+        if down is None and k < 3:
+            hop(k, 1, 0)
+    hash16("pw1", "Ub", [T.neg], 0, 0, 1, ["neg"])
+    op("a", lambda: A.activation(T.cv[:, 1:2], T.pw1[:, 0:1], ACT.Identity), writes=["pw1", "cv"])
     late_y = rank < CFG["late"]
     if not late_y:
         store(0, 0, NC, after=[len(ops) - 1])
+    if down is not None:
+        vhash(1, 0)
+        hash16("pw1", "Vin", [T.neg], 0, 0, 1, ["neg"])
+        op("a", lambda: A.activation(T.cv[:, 0:1], T.pw1[:, 0:1], ACT.Identity), writes=["pw1", "cv"])
+        op("a", lambda: A.activation(T.cv[:, 1:2], T.pw1[:, 0:1], ACT.Identity, bias=T.cv[:, 1:2]), writes=["pw1", "cv"])
+        for k in range(3):
+            hop(k, 1, 0)
 
     def lift(t):
         return 0.0 if t == 1 else LIFT
 
-    def gather(t, a, b, between=None):
+    def gather(t, a, b):
         tab, name = (T.tb, "tb") if t == 1 else (T.tf, "T")
         win = tab[:, 0:W].indirect(T.ho[:, a:b])
         op("v", lambda: V.tensor_tensor(cols(T.s16, t, a, b), win, xc(t, a, b), ALU.add),
            reads=rg(name, 0, NC) + rg("ho", a, b) + xr(t, a, b), writes=sr(t, a, b))
-        if between:
-            between()
+
+    def carry(t, a, b):
         op("v", lambda: V.tensor_scalar(cols(T.k16, t, a, b), cols(T.s16, t, a, b), lift(t) + 256.0, -256.0, ALU.is_ge, ALU.mult),
            reads=sr(t, a, b), writes=kr(t, a, b))
 
-    def total(t, c):
-        a, b = ch[c]
-        bank = "px%d" % (c % 3)
-        pb = T[bank][:, 0:16 * (b - a)]
-        k = op("p", lambda: P.matmul(pb, T.eye[:, :], cols(T.s16, t, a, b), True, False), reads=["eye"] + sr(t, a, b), writes=[bank])
-        op("p", lambda: P.matmul(pb, T.eye[:, :], cols(T.k16, t, a, b), False, True), reads=["eye"] + kr(t, a, b), writes=[bank], group=k)
+    def total(t, parts):
+        heads = [op("p", lambda bk=bk, a=a, b=b: P.matmul(T[bk][:, 0:16 * (b - a)], T.eye[:, :], cols(T.s16, t, a, b), True, False),
+                    reads=["eye"] + sr(t, a, b), writes=[bk]) for bk, a, b in parts]
+        for k, (bk, a, b) in zip(heads, parts):
+            op("p", lambda bk=bk, a=a, b=b: P.matmul(T[bk][:, 0:16 * (b - a)], T.eye[:, :], cols(T.k16, t, a, b), False, True),
+               reads=["eye"] + kr(t, a, b), writes=[bk], group=k)
 
-    def lifted(t, c):
-        a, b = ch[c]
-        bank = "px%d" % (c % 3)
-        op("a", lambda: A.activation(cols(T.xs, 0, a, b), T[bank][:, 0:16 * (b - a)], ACT.Identity, bias=LIFT - lift(t)),
-           reads=[bank], writes=rg("xs", a, b))
-
-    def sample(t, c):
-        a, b = ch[c]
-        bank = "px%d" % (c % 3)
+    def sample(t, bank, a, b):
         op("a", lambda: A.activation(xc(t, a, b), T[bank][:, 0:16 * (b - a)], ACT.Identity, bias=-lift(t)), reads=[bank], writes=xr(t, a, b))
 
     def finish(t, a, b):
         m = a + CFG["fin"]
-        parts = [("pw0", a, m), ("pw1", m, b)]
-        heads = [op("p", lambda n_=n_, lo=lo, hi=hi: P.matmul(T[n_][:, 0:16 * (hi - lo)], T.eye[:, :], cols(T.s16, t, lo, hi), True, False),
-                    reads=["eye"] + sr(t, lo, hi), writes=[n_]) for n_, lo, hi in parts]
-        for k, (n_, lo, hi) in zip(heads, parts):
-            op("p", lambda n_=n_, lo=lo, hi=hi: P.matmul(T[n_][:, 0:16 * (hi - lo)], T.eye[:, :], cols(T.k16, t, lo, hi), False, True),
-               reads=["eye"] + kr(t, lo, hi), writes=[n_], group=k)
-        op("a", lambda: A.activation(xc(t, a, m), T.pw0[:, 0:16 * (m - a)], ACT.Identity, bias=-lift(t)), reads=["pw0"], writes=xr(t, a, m))
+        total(t, [("pw0", a, m), ("pw1", m, b)])
+        sample(t, "pw0", a, m)
         op("v", lambda: V.tensor_scalar(xc(t, m, b), T.pw1[:, 0:16 * (b - m)], -lift(t), None, ALU.add), reads=["pw1"], writes=xr(t, m, b))
 
-    def vhash(t, c):
-        if down is None:
-            return None
+    mark = {}
+
+    def call(what, t, c):
+        if what[-1] == "-":
+            what, c = what[:-1], c - 1
         a, b = ch[c]
-        bank = "pv%d" % (c % 2)
-        hash16(bank, "Vin", T.Z, (t - 1) * S, a, b, rg("Z%d" % t, a, b))
-        return bank
-
-    def scatters(t, place, e):
-        for a, b, pe, pl in pieces:
-            if pl == place and pe == e:
-                scatter(e, t, a, b)
-
-    bank = vhash(1, 0)
-    if down is not None and CFG["cv_late"]:
-        lift_v()
-    for t in range(1, M):
-        more = t < M - 1
-        ks = None
-        for c, (a, b) in enumerate(ch):
-            weave = more and c == last and w1 < a and down is not None
-            if weave:
-                hops(t, a, b, bank, lambda k: wops("pw0", "jf1", 0, w1, (k,)))
-            elif down is not None:
-                hops(t, a, b, bank)
-            if c < last:
-                bank = vhash(t, c + 1)
-            mix = more and c == CFG["wops_at"] and down is not None and CFG["mix"] and not weave
-            gather(t, a, b, (lambda: wops("pw0", "jf1", 0, w1, (0,))) if mix else None)
+        half, bank, more = (a + b) // 2, "px%d" % (c % 3), t < M - 1
+        nt, nc = (t, c + 1) if c < last else (t + 1, 0)
+        if what == "G":
+            gather(t, a, b)
+        elif what in ("G1", "G2"):
+            gather(t, *((a, half & ~1) if what == "G1" else (half & ~1, b)))
+        elif what == "K":
+            carry(t, a, b)
+        elif what in ("K1", "K2"):
+            carry(t, *((a, half & ~1) if what == "K1" else (half & ~1, b)))
+        elif what in ("A", "B", "C"):
+            hop("ABC".index(what), nt, nc)
+        elif what == "hv":
+            vhash(nt, nc)
+        elif what == "send":
             if up is not None:
-                ks = send(t, c)
+                mark["send"] = send(t, c)
             if t == 1 and c == last and wide < NC:
                 op("v", lambda: V.tensor_scalar(T.tf[:, 64 * wide:W], T.tb[:, 64 * wide:W], LIFT, None, ALU.add), reads=rg("tb", wide, NC), writes=rg("T", wide, NC))
-            if more and c == CFG["wops_at"] and not weave:
-                wops("pw0", "jf1", 0, w1, (1, 2) if mix else (0, 1, 2))
-            if up is None and c == last and not more:
-                finish(t, a, b)
-            elif c < last or not more:
-                total(t, c)
-                if more and b == w1:
-                    hash16("pw0", "Wb", T.s16, t * S, 0, w1, sr(t, 0, w1))
-                if more:
-                    lifted(t, c)
-                sample(t, c)
+        elif what == "sum":
+            total(t, [(bank, a, b)])
+        elif what == "x":
+            sample(t, bank, a, b)
             if not more and up is None:
                 store(t, a, b)
+        elif not more:
+            pass
+        elif what == "xs":
+            op("a", lambda: A.activation(cols(T.xs, 0, a, b), T[bank][:, 0:16 * (b - a)], ACT.Identity, bias=LIFT - lift(t)), reads=[bank], writes=rg("xs", a, b))
+        elif what == "wa":
+            if b == w1:
+                hash16("pw0", "Wb", [T.s16], t * S, 0, w1, sr(t, 0, w1))
+        elif what == "wb":
+            hash16("pw1", "Wb", [T.s16], t * S, w1, NC, sr(t, w1, NC))
+        elif what[0] == "p":
+            wop(int(what[1]), "pw0", "jf1", 0, w1)
+        elif what[0] == "q":
+            wop(int(what[1]), "pw1", "jf1", w1, NC)
+        elif what == "u":
+            hash16("pu", "Ub", [T.s16, T.k16], t * S, 0, NC, sr(t, 0, NC) + kr(t, 0, NC))
+        elif what == "us":
+            uevac(t)
+        elif what == "ua":
+            if down is not None:
+                hash16("pu", "Ub", [T.s16, T.k16], t * S, 0, b, sr(t, 0, b) + kr(t, 0, b))
+        elif what == "usa":
+            uevac(t, "pu", 0, ch[last][0])
+        elif what == "ub":
+            bk, lo = ("pu", 0) if down is None else ("pw1", a)
+            hash16(bk, "Ub", [T.s16, T.k16], t * S, lo, NC, sr(t, lo, NC) + kr(t, lo, NC))
+        elif what == "usb":
+            uevac(t, "pw1", ch[last][0], NC)
+        elif what == "gate":
+            mark["gate"] = len(ops) - 1
+        else:
+            scatter(t, what)
+
+    for t in range(1, M):
+        more = t < M - 1
+        for c, (a, b) in enumerate(ch):
+            for what in CFG["order"][c].split():
+                call(what, t, c)
+        if not more and up is None:
+            finish(t, a, b)
+            store(t, a, b)
         if more:
-            for what in CFG["end"]:
-                if what == "sum":
-                    total(t, last)
-                elif what == "xs":
-                    lifted(t, last)
-                elif what == "x":
-                    sample(t, last)
-                elif what == "w":
-                    hash16("pw1", "Wb", T.s16, t * S, w1, NC, sr(t, w1, NC))
-                elif what == "wo":
-                    wops("pw1", "jf1", w1, NC)
-                elif what == "u":
-                    hash16("pu", "Ub", T.s16, t * S, 0, NC, sr(t, 0, NC) + kr(t, 0, NC), [("Ub", T.k16)])
-                elif what in ("u0", "us0", "us1") and down is None:
-                    pass
-                elif what == "u1" and down is None:
-                    hash16("pu", "Ub", T.s16, t * S, 0, NC, sr(t, 0, NC) + kr(t, 0, NC), [("Ub", T.k16)])
-                elif what == "u0":
-                    hash16("pu", "Ub", T.R, t * S, 0, first, xr(t, 0, first))
-                elif what == "us0":
-                    op("a", lambda: A.activation(T.us[:, 0:first], T.pu[:, 0:first], ACT.Identity, bias=T.cv[:, 0:1]), reads=["cv"], writes=["pu"] + rg("us", 0, first))
-                elif what == "u1":
-                    hash16("pw0", "Ub", T.s16, t * S, first, NC, sr(t, first, NC) + kr(t, first, NC), [("Ub", T.k16)])
-                elif what == "us1":
-                    op("a", lambda t=t: A.activation(T.us[:, first:NC], T.pw0[:, 0:NC - first], ACT.Identity, bias=T.cv[:, 0:1] if t == 1 else T.cv[:, 1:2]),
-                       reads=["cv"], writes=["pw0"] + rg("us", first, NC))
-                elif what == "ux":
-                    hash16("pu", "Ub", T.R, t * S, 0, NC, xr(t, 0, NC))
-                elif what == "v":
-                    bank = vhash(t + 1, 0)
-                elif what == "us":
-                    if down is not None:
-                        uevac(t)
-                else:
-                    scatters(t, int(what[1]), what[0])
-                if what == CFG["gate"]:
-                    gate = [len(ops) - 1]
-            if down is None:
-                hops(t + 1, 0, NC)
+            for what in CFG["end"].split():
+                call(what, t, last)
+        elif up is not None:
+            call("sum", t, last)
+            call("x", t, last)
         left = []
         if up is not None:
-            left = [ext("sent%d" % t, ucnt * len(ch), kn=ops[ks]["kn"])]
+            left = [ext("sent%d" % t, ucnt * len(ch), kn=ops[mark["send"]]["kn"])]
             ends.extend(left)
         if more:
-            if CFG["gate"] is None:
-                gate = left
             for _ in range(2):
                 if todo:
-                    load_res(*todo.pop(0), after=gate)
+                    load_res(*todo.pop(0), after=[mark["gate"]])
             if not late_y:
-                store(t, 0, NC, after=gate)
+                store(t, 0, NC, after=[mark["gate"]])
         elif up is not None:
             if late_y:
                 for tt in range(M - 1):

from concourse.bass import DstId, RemoteDMATransfer
from concourse.mybir import AluOpType as ALU, ActivationFunctionType as ACT

S, M, W, NC = 1024, 5, 4096, 64
LIFT = 256.0

CFG = {
    "chunks": [0, 22, 44, 64],
    "w1": 22,
    "pieces": [(0, 10, "a1"), (10, 16, "v1"), (16, 18, "v2"), (18, 20, "v3"), (20, 22, "v4"), (22, 40, "v5"), (40, 42, "v6"),
               (42, 44, "v7"), (44, 54, "a2"), (54, 64, "a3")],
    "order": ["hv G1 G2 wa K1 A K2 send B C", "hv sum- xs- x- G1 G2 K1 A K2 send p0 B p1 C p2 sum xs x", "G K send"],
    "end": "a1 wb sum v1 q0 v2 q1 v3 q2 gate v4 xs u hv a2 us a3 v5 A v6 B v7 C x",
    "tab": [(0, 16), (16, 36), (36, 56), (56, 64)],
    "late": 4,
    "fin": 10,
    "wide0": 56,
    "early": (2, 3),
}
MAXC = 6

SCRATCH = {
    "R": ("sbuf", [128, M * S], "bfloat16"),
    "Z": ("sbuf", [128, (M - 1) * S], "float16"),
    "Vin": ("sbuf", [128, 144], "bfloat16"),
    "us": ("sbuf", [128, NC], "float32"),
    "tb": ("sbuf", [128, W], "bfloat16"),
    "tf": ("sbuf", [128, W], "float32"),
    "hwb": ("sbuf", [128, 8], "bfloat16"),
    "Ub": ("sbuf", [128, 144], "bfloat16"),
    "Wb": ("sbuf", [128, 144], "bfloat16"),
    "Vb": ("sbuf", [128, 144], "bfloat16"),
    "one": ("sbuf", [128, 128], "bfloat16"),
    "eye": ("sbuf", [128, 128], "bfloat16"),
    "neg": ("sbuf", [128, 16], "bfloat16"),
    "cv": ("sbuf", [128, 4], "float32"),
    "i8": ("sbuf", [128, 8], "int32"),
    "m8": ("sbuf", [128, 8], "float32"),
    "p4i": ("sbuf", [128, 4], "int32"),
    "p4f": ("sbuf", [128, 4], "float32"),
    "jc": ("sbuf", [128, NC], "int32"),
    "jf0": ("sbuf", [128, NC], "float32"),
    "jf1": ("sbuf", [128, NC], "float32"),
    "s16": ("sbuf", [128, M * S], "float16"),
    "k16": ("sbuf", [128, M * S], "float16"),
    "xs": ("sbuf", [128, S], "float32"),
    "ha": ("sbuf", [128, NC], "int32"),
    "ho": ("sbuf", [128, NC], "uint16"),
    "wa": ("sbuf", [128, NC], "int32"),
    "wf": ("sbuf", [128, NC], "float32"),
    "wo": ("sbuf", [128, NC], "uint16"),
    "pv0": ("psum", [128, 512], "float32"),
    "pv1": ("psum", [128, 512], "float32"),
    "pw0": ("psum", [128, 512], "float32"),
    "pw1": ("psum", [128, 512], "float32"),
    "pu": ("psum", [128, 512], "float32"),
    "px0": ("psum", [128, 512], "float32"),
    "px1": ("psum", [128, 512], "float32"),
    "px2": ("psum", [128, 512], "float32"),
}
POOL = {"d": 34, "v": 26, "a": 22, "p": 22, "g": 14}
SEMAPHORES = ([k + str(i) for k in POOL for i in range(POOL[k])]
              + ["z%d_%d" % (t, c) for t in range(1, M) for c in range(MAXC)] + ["vin"] + ["sent%d" % t for t in range(M)])


def rg(name, a, b):
    return [(name, c) for c in range(a, b)]


def emit(g, T, ops):
    queues = {"g": g, "v": g.vector, "a": g.scalar, "p": g.tensor, "s": g.sync}
    last, total = {}, {}
    for k, o in enumerate(ops):
        if o["tok"] is None and o["waited"]:
            pool = "d" if o["dma"] else o["q"]
            for i in range(POOL[pool]):
                s = pool + str(i)
                if s not in last or o["kn"] >> last[s] & 1:
                    break
            else:
                raise ValueError("out of semaphores in pool " + pool)
            last[s] = k
            total[s] = total.get(s, 0) + (16 if o["dma"] else 1)
            o["tok"] = (s, total[s])
            o["inc"] = True
    for o in ops:
        if o["q"] is None:
            continue
        q = queues[o["q"]]
        for d in o["waits"]:
            q.wait_ge(T.sem[ops[d]["tok"][0]], ops[d]["tok"][1])
        if o["fn"] is not None:
            ins = o["fn"]()
            if o["inc"]:
                ins.then_inc(T.sem[o["tok"][0]], 16 if o["dma"] else 1)


def rank_program(g, core, T, topo):
    rank = T.rank_of(core)
    if rank is None:
        return
    n = len(T.cores)
    up = T.cores[rank + 1] if rank + 1 < n else None
    down = T.cores[rank - 1] if rank > 0 else None
    ch = list(zip(CFG["chunks"], CFG["chunks"][1:]))
    w1, pieces, tabp = CFG["w1"], CFG["pieces"], CFG["tab"]
    last = len(ch) - 1

    ops, known, writer, readers = [], {}, {}, {}

    def op(q, fn, reads=(), writes=(), dma=False, after=(), group=None):
        k = len(ops)
        deps = set(after)
        for r in reads:
            if r in writer:
                deps.add(writer[r])
        for r in writes:
            if r in writer:
                deps.add(writer[r])
            deps.update(readers.get(r, ()))
        deps.discard(group)
        kn, waits = known.get(q, 0), []
        for d in sorted(deps, reverse=True):
            if not kn >> d & 1:
                waits.append(d)
                ops[d]["waited"] = True
                kn |= ops[d]["kn"] | 1 << d
        known[q] = kn
        ops.append({"q": q, "fn": fn, "waits": waits[::-1], "kn": kn, "dma": dma, "waited": False, "tok": None, "inc": False})
        for r in reads:
            readers.setdefault(r, []).append(k)
        for r in writes:
            writer[r] = k
            readers[r] = []
        return k

    def ext(sem, val, writes=(), kn=0):
        k = len(ops)
        ops.append({"q": None, "fn": None, "waits": [], "kn": kn, "dma": False, "waited": False, "tok": (sem, val), "inc": False})
        for r in writes:
            writer[r] = k
            readers[r] = []
        return k

    V, A, P, Y = g.vector, g.scalar, g.tensor, g.sync
    ends = []

    def xr(t, a, b):
        return rg("R%d" % t, a, b)

    def sr(t, a, b):
        return rg("s%d" % t, a, b)

    def kr(t, a, b):
        return rg("k%d" % t, a, b)

    def cols(buf, t, a, b):
        return buf[:, t * S + 16 * a:t * S + 16 * b]

    def xc(t, a, b):
        return cols(T.R, t, a, b)

    def load(q, out, in_, writes, after=()):
        e = A if q == "a" else Y
        return op(q, lambda: e.dma_start(out, in_), writes=writes, dma=True, after=after)

    def load_res(t, a, b, after=()):
        load("s", xc(t, a, b), cols(T.res, t, a, b), xr(t, a, b), after)

    def store(t, a, b, after=()):
        ends.append(op("s", lambda: Y.dma_start(cols(T.y, t, a, b), xc(t, a, b)), reads=xr(t, a, b), dma=True, after=after))

    def hash16(bank, band, srcs, base, a, b, reads):
        def fn():
            ins = None
            for k, src in enumerate(srcs):
                for p in range(16):
                    ins = P.matmul(T[bank][:, 0:b - a], T[band][:, 15 - p:143 - p], src[:, base + 16 * a + p:base + 16 * b:16],
                                   k == 0 and p == 0, k == len(srcs) - 1 and p == 15)
            return ins
        return op("p", fn, reads=list(reads) + [band], writes=[bank])

    load("a", T.hwb[:, 0:3], T.hw[:, 0:3], ["hw"])
    load_res(0, 0, NC)
    for a, b in tabp:
        load("s", T.tb[:, 64 * a:64 * b], T.tab[:, 64 * a:64 * b], rg("tb", a, b))
    cut = [0, ch[0][1], NC] if down is None else [0, NC]
    todo = [(t, a, b) for t in range(1, M) for a, b in zip(cut, cut[1:])]
    for _ in range(CFG["early"][rank] if rank < len(CFG["early"]) else M - 1):
        load_res(*todo.pop(0))

    op("g", lambda: g.iota(T.i8[:, 0:8], [[-16, 8]], 0, 1), writes=["i8"])
    op("g", lambda: g.iota(T.p4i[:, 0:1], [[0, 1]], 0, 1), writes=["p4i"])
    op("g", lambda: g.iota(T.jc[:, :], [[16, NC]], 0, 0), writes=["jc"])

    def streams(jf, windows):
        for a, b in windows:
            op("v", lambda a=a, b=b: V.tensor_scalar(T[jf][:, a:b], T.jc[:, a:b], T.p4f[:, 0:1], -16.0 * a, ALU.add, ALU.add), reads=["jc", "p4f"], writes=rg(jf, a, b))

    bands = [("Wb", 2), ("Ub", 0)] + ([("Vb", 1)] if up is not None else [])
    for nm, _k in bands:
        op("v", lambda nm=nm: V.memset(T[nm][:, :], 0.0), writes=[nm])
    op("v", lambda: V.memset(T.one[:, :], 1.0), writes=["one"])
    op("v", lambda: V.memset(T.neg[:, :], -LIFT), writes=["neg"])
    op("v", lambda: V.tensor_scalar(T.i8[:, 0:8], T.i8[:, 0:8], 4, None, ALU.arith_shift_right), reads=["i8"], writes=["i8"])
    op("v", lambda: V.tensor_scalar(T.p4i[:, 0:1], T.p4i[:, 0:1], 15, None, ALU.bitwise_and), reads=["p4i"], writes=["p4i"])
    op("v", lambda: V.tensor_scalar(T.m8[:, 0:8], T.i8[:, 0:8], 0.0, None, ALU.is_equal), reads=["i8"], writes=["m8"])
    op("v", lambda: V.tensor_scalar(T.p4f[:, 0:1], T.p4i[:, 0:1], 0.375, None, ALU.add), reads=["p4i"], writes=["p4f"])
    streams("jf0", tabp)
    for nm, k in bands:
        op("v", lambda nm=nm, k=k: V.tensor_scalar(T[nm][:, 15:128:16], T.m8[:, 0:8], T.hwb[:, k:k + 1], 0.25 if nm == "Wb" else 1.0, ALU.mult, ALU.mult),
           reads=["m8", "hw"], writes=[nm])
    op("g", lambda: g.affine_select(T.eye[:, :], T.one[:, :], [[-1, 128]], ALU.is_equal, 0.0, 0, 1), reads=["one"], writes=["eye"])
    streams("jf1", [pc[:2] for pc in pieces])

    if up is not None:
        rid, pid, _se = topo.addr(up)
        umask, ucnt = topo.mask(core, up), len(topo.engines(core, up))
        k = op("g", lambda: g.remote_dma(T.Vin[:, :], T.Vb[:, :], T.sem["vin"], T.sem["sent0"], pid, rid, umask), reads=["Vb"])
        ends.append(ext("sent0", ucnt, kn=ops[k]["kn"]))
    if down is not None:
        dcnt = len(topo.engines(down, core))
        ext("vin", dcnt, writes=["Vin"])
        for t in range(1, M):
            for c, (a, b) in enumerate(ch):
                ext("z%d_%d" % (t, c), dcnt, writes=rg("Z%d" % t, a, b))

    def send(t, c):
        a, b = ch[c]
        tr = RemoteDMATransfer(dst_ids=[DstId(rid=rid, pnc=pid)], dma_engine_mask=umask, remote_sem=T.sem["z%d_%d" % (t, c)],
                               srcs=[cols(T.s16, t, a, b), cols(T.k16, t, a, b)], dsts=[cols(T.Z, t - 1, a, b)], alu_op=1)
        return op("g", lambda: g.remote_dma_fused([tr], local_sem=T.sem["sent%d" % t]), reads=sr(t, a, b) + kr(t, a, b))

    def wop(k, bank, jf, a, b):
        pb = T[bank][:, 0:b - a]
        if k == 0:
            op("v", lambda: V.tensor_tensor(T.wa[:, a:b], pb, T[jf][:, a:b], ALU.subtract), reads=rg(jf, a, b), writes=[bank] + rg("wa", a, b))
        elif k == 1:
            op("v", lambda: V.tensor_tensor(T.wf[:, a:b], pb, T.wa[:, a:b], ALU.subtract), reads=rg("wa", a, b), writes=[bank] + rg("wf", a, b))
        else:
            op("v", lambda: V.tensor_scalar(T.wo[:, a:b], T.wf[:, a:b], 4.0, None, ALU.mult), reads=rg("wf", a, b), writes=rg("wo", a, b))

    def hop(k, t, c):
        a, b = ch[c]
        if down is None:
            if c > 0:
                return
            b = NC
        if k == 1:
            op("v", lambda: V.tensor_scalar(T.ha[:, a:b], T.ha[:, a:b], W - 1, None, ALU.bitwise_and), writes=rg("ha", a, b))
        elif k == 2:
            op("v", lambda: V.tensor_copy(T.ho[:, a:b], T.ha[:, a:b]), reads=rg("ha", a, b), writes=rg("ho", a, b))
        elif down is not None:
            bank = "pv%d" % (c % 2)
            op("v", lambda: V.tensor_tensor(T.ha[:, a:b], T[bank][:, 0:b - a], T.us[:, a:b], ALU.add), reads=rg("us", a, b), writes=[bank] + rg("ha", a, b))
        elif t <= 2:
            op("v", lambda: V.tensor_copy(T.ha[:, a:b], T.pu[:, a:b]), writes=["pu"] + rg("ha", a, b))
        else:
            op("v", lambda: V.tensor_scalar(T.ha[:, a:b], T.pu[:, a:b], T.cv[:, 1:2], None, ALU.add), reads=["cv"], writes=["pu"] + rg("ha", a, b))

    def scatter(t, name):
        for a, b, nm in pieces:
            if nm == name:
                out, src = T.tf[:, 64 * a:64 * b].indirect(T.wo[:, a:b]), cols(T.xs, 0, a, b)
                fn = (lambda out=out, src=src: A.activation(out, src, ACT.Silu)) if nm[0] == "a" else (lambda out=out, src=src: V.tensor_copy(out, src))
                op(nm[0], fn, reads=rg("xs", a, b) + rg("wo", a, b), writes=rg("T", a, b))

    def uevac(t, bank="pu", a=0, b=NC):
        if down is not None:
            bias = 0.0 if t == 0 else T.cv[:, 0:1] if t == 1 else T.cv[:, 1:2]
            op("a", lambda: A.activation(T.us[:, a:b], T[bank][:, 0:b - a], ACT.Identity, bias=bias), reads=["cv"] if t else [], writes=[bank] + rg("us", a, b))

    def vhash(t, c):
        if down is not None:
            a, b = ch[c]
            hash16("pv%d" % (c % 2), "Vin", [T.Z], (t - 1) * S, a, b, rg("Z%d" % t, a, b))

    hash16("pw0", "Wb", [T.R], 0, 0, NC, xr(0, 0, NC))
    hash16("pu", "Ub", [T.R], 0, 0, NC, xr(0, 0, NC))
    for k in range(3):
        wop(k, "pw0", "jf0", 0, NC)
    uevac(0)
    wide = CFG["wide0"] if down is None else NC
    for k, (a, b) in enumerate(tabp):
        op("v", lambda a=a, b=b: V.tensor_copy(T.tb[:, 64 * a:64 * b].indirect(T.wo[:, a:b]), xc(0, a, b)),
           reads=xr(0, a, b) + rg("wo", a, b), writes=rg("tb", a, b))
        b = min(b, wide)
        if a < b:
            op("a", lambda a=a, b=b: A.activation(T.tf[:, 64 * a:64 * b], T.tb[:, 64 * a:64 * b], ACT.Silu, bias=LIFT), reads=rg("tb", a, b), writes=rg("T", a, b))
        if down is None and k < 3:
            hop(k, 1, 0)
    hash16("pw1", "Ub", [T.neg], 0, 0, 1, ["neg"])
    op("a", lambda: A.activation(T.cv[:, 1:2], T.pw1[:, 0:1], ACT.Identity), writes=["pw1", "cv"])
    late_y = rank < CFG["late"]
    if not late_y:
        store(0, 0, NC, after=[len(ops) - 1])
    if down is not None:
        vhash(1, 0)
        hash16("pw1", "Vin", [T.neg], 0, 0, 1, ["neg"])
        op("a", lambda: A.activation(T.cv[:, 0:1], T.pw1[:, 0:1], ACT.Identity), writes=["pw1", "cv"])
        op("a", lambda: A.activation(T.cv[:, 1:2], T.pw1[:, 0:1], ACT.Identity, bias=T.cv[:, 1:2]), writes=["pw1", "cv"])
        for k in range(3):
            hop(k, 1, 0)

    def lift(t):
        return 0.0 if t == 1 else LIFT

    def gather(t, a, b):
        tab, name = (T.tb, "tb") if t == 1 else (T.tf, "T")
        win = tab[:, 0:W].indirect(T.ho[:, a:b])
        op("v", lambda: V.tensor_tensor(cols(T.s16, t, a, b), win, xc(t, a, b), ALU.add),
           reads=rg(name, 0, NC) + rg("ho", a, b) + xr(t, a, b), writes=sr(t, a, b))

    def carry(t, a, b):
        op("v", lambda: V.tensor_scalar(cols(T.k16, t, a, b), cols(T.s16, t, a, b), lift(t) + 256.0, -256.0, ALU.is_ge, ALU.mult),
           reads=sr(t, a, b), writes=kr(t, a, b))

    def total(t, parts):
        heads = [op("p", lambda bk=bk, a=a, b=b: P.matmul(T[bk][:, 0:16 * (b - a)], T.eye[:, :], cols(T.s16, t, a, b), True, False),
                    reads=["eye"] + sr(t, a, b), writes=[bk]) for bk, a, b in parts]
        for k, (bk, a, b) in zip(heads, parts):
            op("p", lambda bk=bk, a=a, b=b: P.matmul(T[bk][:, 0:16 * (b - a)], T.eye[:, :], cols(T.k16, t, a, b), False, True),
               reads=["eye"] + kr(t, a, b), writes=[bk], group=k)

    def sample(t, bank, a, b):
        op("a", lambda: A.activation(xc(t, a, b), T[bank][:, 0:16 * (b - a)], ACT.Identity, bias=-lift(t)), reads=[bank], writes=xr(t, a, b))

    def finish(t, a, b):
        m = a + CFG["fin"]
        total(t, [("pw0", a, m), ("pw1", m, b)])
        sample(t, "pw0", a, m)
        op("v", lambda: V.tensor_scalar(xc(t, m, b), T.pw1[:, 0:16 * (b - m)], -lift(t), None, ALU.add), reads=["pw1"], writes=xr(t, m, b))

    mark = {}

    def call(what, t, c):
        if what[-1] == "-":
            what, c = what[:-1], c - 1
        a, b = ch[c]
        half, bank, more = (a + b) // 2, "px%d" % (c % 3), t < M - 1
        nt, nc = (t, c + 1) if c < last else (t + 1, 0)
        if what == "G":
            gather(t, a, b)
        elif what in ("G1", "G2"):
            gather(t, *((a, half & ~1) if what == "G1" else (half & ~1, b)))
        elif what == "K":
            carry(t, a, b)
        elif what in ("K1", "K2"):
            carry(t, *((a, half & ~1) if what == "K1" else (half & ~1, b)))
        elif what in ("A", "B", "C"):
            hop("ABC".index(what), nt, nc)
        elif what == "hv":
            vhash(nt, nc)
        elif what == "send":
            if up is not None:
                mark["send"] = send(t, c)
            if t == 1 and c == last and wide < NC:
                op("v", lambda: V.tensor_scalar(T.tf[:, 64 * wide:W], T.tb[:, 64 * wide:W], LIFT, None, ALU.add), reads=rg("tb", wide, NC), writes=rg("T", wide, NC))
        elif what == "sum":
            total(t, [(bank, a, b)])
        elif what == "x":
            sample(t, bank, a, b)
            if not more and up is None:
                store(t, a, b)
        elif not more:
            pass
        elif what == "xs":
            op("a", lambda: A.activation(cols(T.xs, 0, a, b), T[bank][:, 0:16 * (b - a)], ACT.Identity, bias=LIFT - lift(t)), reads=[bank], writes=rg("xs", a, b))
        elif what == "wa":
            if b == w1:
                hash16("pw0", "Wb", [T.s16], t * S, 0, w1, sr(t, 0, w1))
        elif what == "wb":
            hash16("pw1", "Wb", [T.s16], t * S, w1, NC, sr(t, w1, NC))
        elif what[0] == "p":
            wop(int(what[1]), "pw0", "jf1", 0, w1)
        elif what[0] == "q":
            wop(int(what[1]), "pw1", "jf1", w1, NC)
        elif what == "u":
            hash16("pu", "Ub", [T.s16, T.k16], t * S, 0, NC, sr(t, 0, NC) + kr(t, 0, NC))
        elif what == "us":
            uevac(t)
        elif what == "ua":
            if down is not None:
                hash16("pu", "Ub", [T.s16, T.k16], t * S, 0, b, sr(t, 0, b) + kr(t, 0, b))
        elif what == "usa":
            uevac(t, "pu", 0, ch[last][0])
        elif what == "ub":
            bk, lo = ("pu", 0) if down is None else ("pw1", a)
            hash16(bk, "Ub", [T.s16, T.k16], t * S, lo, NC, sr(t, lo, NC) + kr(t, lo, NC))
        elif what == "usb":
            uevac(t, "pw1", ch[last][0], NC)
        elif what == "gate":
            mark["gate"] = len(ops) - 1
        else:
            scatter(t, what)

    for t in range(1, M):
        more = t < M - 1
        for c, (a, b) in enumerate(ch):
            for what in CFG["order"][c].split():
                call(what, t, c)
        if not more and up is None:
            finish(t, a, b)
            store(t, a, b)
        if more:
            for what in CFG["end"].split():
                call(what, t, last)
        elif up is not None:
            call("sum", t, last)
            call("x", t, last)
        left = []
        if up is not None:
            left = [ext("sent%d" % t, ucnt * len(ch), kn=ops[mark["send"]]["kn"])]
            ends.extend(left)
        if more:
            for _ in range(2):
                if todo:
                    load_res(*todo.pop(0), after=[mark["gate"]])
            if not late_y:
                store(t, 0, NC, after=[mark["gate"]])
        elif up is not None:
            if late_y:
                for tt in range(M - 1):
                    store(tt, 0, NC, after=left)
            store(t, 0, NC, after=left)
    op("s", None, after=ends)
    emit(g, T, ops)
